import numpy as np
import ml_dtypes


def mxq(x, axis, fmt="e4m3"):
    dtype, down = {"e4m3": (ml_dtypes.float8_e4m3fn, 7), "e5m2": (ml_dtypes.float8_e5m2, 14)}[fmt]
    v = np.moveaxis(np.asarray(x, np.float32).astype(ml_dtypes.bfloat16).astype(np.float64), axis, -1)
    blocks = v.reshape(v.shape[:-1] + (-1, 32))
    amax = np.abs(blocks).max(-1, keepdims=True)
    byte = np.maximum(np.where(amax > 0, np.frexp(amax)[1] - 1 + 127, 0) - down, 1)
    scale = np.exp2(byte - 127.0)
    codes = (blocks / scale).astype(np.float32).astype(dtype).astype(np.float64)
    return np.moveaxis((codes * scale).reshape(v.shape), -1, axis)


WIDE = False


def mx_kscale(k):
    if not WIDE:
        return np.ones(k)
    levels = np.array([18, -18])
    if k % 512:
        return np.exp2(np.random.permutation(np.resize(levels, k // 32))).repeat(32)
    a = np.empty((k // 512, 16))
    for p in range(k // 512):
        a[p, :8] = np.random.permutation(np.resize(levels, 8))
        for g in range(8):
            far = levels[np.abs(levels - a[p, g]) >= 10]
            a[p, g + 8] = far[np.random.randint(len(far))]
    return np.exp2(a.ravel()).repeat(32)


def f64(x):
    return np.asarray(x).astype(np.float64)


def striped(idx):
    return np.tile(np.asarray(idx).reshape(-1, 16).T, (8, 1)).astype(np.uint16)


def unstriped(offs):
    return offs[:16].T.reshape(-1).astype(np.int64)


B, N, T, D, R, TU = 1, 512, 2048, 512, 1024, 2048


def setup_inputs():
    n = np.random.standard_normal
    idx = np.random.permutation(T)[:B * N]
    uidx = np.random.permutation(TU)[:B * R]
    s = mx_kscale(D)[:, None]
    z = np.ones(TU)
    z[uidx] = mx_kscale(B * R)
    u = np.ones(T)
    u[idx] = mx_kscale(B * N)
    r = np.random.uniform(0.5, 2.0, T) * u
    ur = np.random.uniform(0.5, 2.0, TU) * z
    return {
        "uT": (n((D, TU)) * s / ur).astype(np.float32),
        "vT": (n((D, T)) * (1.00 / np.sqrt(D)) / s / r).astype(np.float32),
        "y": n((B, R, N)).astype(np.float32),
        "us": ur[uidx].reshape(B, R, 1).astype(np.float32),
        "ts": np.tile(r, (128, 1)).astype(np.float32),
        "kb": np.tile(0.5 * n(T), (128, 1)).astype(np.float32),
        "offs": striped(idx),
        "uoffs": striped(uidx),
    }


def reference(uT, vT, y, us, ts, kb, offs, uoffs):
    idx = unstriped(offs)
    pick = lambda x: x[:, idx].reshape(x.shape[0], B, N).transpose(1, 0, 2)
    uidx = unstriped(uoffs)
    w = pick(f64(vT))
    x = f64(uT)[:, uidx].reshape(D, B, R).transpose(1, 0, 2)
    a = mxq(x, 1, "e4m3").transpose(0, 2, 1) @ mxq(w, 1, "e4m3")
    sc = f64(us) * pick(f64(ts))[:, :1, :]
    a = a * sc
    a = a + pick(f64(kb))[:, :1, :]
    g = (a - f64(y))
    h = sc * g
    dv = mxq(x, 2, "e4m3") @ mxq(h, 1, "e5m2")
    gv = np.zeros((D, T))
    gv[:, idx] = dv.transpose(1, 0, 2).reshape(D, B * N)
    return gv

@@ -1,0 +1,277 @@
+from contextlib import ExitStack
+
+import concourse.mybir as mybir
+from concourse.masks import make_identity
+
+D, T, TU, N, R = 512, 2048, 2048, 512, 1024
+P = 128
+PACK = 4
+PASS = P * PACK
+G = R // PASS
+NB = N // P
+HALF = N // 2
+
+FLOPS = 2 * 2 * R * N * D
+BYTES = 4 * (D * TU + D * T + R * N + R + 2 * T + D * T) + 2 * P * (N + R) // 16
+
+F32 = mybir.dt.float32
+BF16 = mybir.dt.bfloat16
+U32 = mybir.dt.uint32
+U16 = mybir.dt.uint16
+U8 = mybir.dt.uint8
+E4M3 = mybir.dt.float8_e4m3fn_x4
+E5M2 = mybir.dt.float8_e5m2_x4
+ALU = mybir.AluOpType
+COPY = mybir.ActivationFunctionType.Copy
+
+
+def tile_attend_gmf_sq_v_kb_kernel(tc, uT, vT, y, us, ts, kb, offs, uoffs, out):
+    nc = tc.nc
+    with ExitStack() as ctx:
+        keep = ctx.enter_context(tc.tile_pool(name="keep", bufs=1))
+        work = ctx.enter_context(tc.tile_pool(name="work", bufs=2))
+        psum = ctx.enter_context(tc.psum_pool(name="psum", bufs=2))
+
+        ts_win = keep.tile([P, T], F32, name="ts_win")
+        kb_win = keep.tile([P, T], F32, name="kb_win")
+        nc.gpsimd.memset(ts_win[:, :T // 2], 0.0)
+        nc.vector.memset(ts_win[:, T // 2:], 0.0)
+        nc.vector.memset(kb_win[:], 0.0)
+        ident = keep.tile([P, P], F32, name="ident")
+        make_identity(nc, ident[:])
+
+        items = keep.tile([P, N // 16], U16, name="items")
+        users = keep.tile([P, R // 16], U16, name="users")
+        us_col = keep.tile([P, G, PACK], F32, name="us_col")
+        u_planes = uT.rearrange("(p j) c -> j p c", j=PACK)
+        v_planes = vT.rearrange("(p j) c -> j p c", j=PACK)
+        u_win = [keep.tile([P, TU], F32, name=f"u_win{j}") for j in range(PACK)]
+        v_win = [keep.tile([P, T], F32, name=f"v_win{j}") for j in range(PACK)]
+        nc.sync.dma_start(out=u_win[0][:], in_=u_planes[0])
+        nc.sync.dma_start(users[:], uoffs)
+        nc.sync.dma_start(items[:], offs)
+        nc.sync.dma_start(out=ts_win[0:1, :], in_=ts[0:1, :])
+        nc.sync.dma_start(out=us_col[:], in_=us[0].rearrange("(g s t) o -> s g (t o)", g=G, t=PACK))
+        nc.sync.dma_start(out=u_win[1][:], in_=u_planes[1])
+        nc.sync.dma_start(out=kb_win[0:1, :], in_=kb[0:1, :])
+        for j in range(2, PACK):
+            nc.sync.dma_start(out=u_win[j][:], in_=u_planes[j])
+        for j in range(PACK):
+            nc.sync.dma_start(out=v_win[j][:], in_=v_planes[j])
+        y_sb = {}
+        for h in range(2):
+            for g in range(G):
+                y_sb[(h, g)] = keep.tile([P, PACK, HALF], F32, name=f"y_sb{h}_{g}")
+                nc.sync.dma_start(out=y_sb[(h, g)][:],
+                                  in_=y[0, g * PASS:(g + 1) * PASS, h * HALF:(h + 1) * HALF].rearrange("(s t) i -> s t i", t=PACK))
+
+        out_win = [keep.tile([P, T], F32, name=f"out_win{j}") for j in range(PACK)]
+        for j in range(PACK):
+            nc.gpsimd.memset(out_win[j][:], 0.0)
+
+        def column_of(name, win):
+            picked = keep.tile([P, N], F32, name=f"{name}_picked")
+            nc.vector.tensor_copy(picked[:], win[:].indirect(items[:]))
+            turned = psum.tile([P, NB, P], F32, name="turned", tag="h_bank")
+            for b in range(NB):
+                nc.tensor.transpose(turned[:, b, :], picked[:, b * P:(b + 1) * P], ident[:])
+            col = keep.tile([P, NB], F32, name=f"{name}_col")
+            nc.scalar.copy(out=col[:], in_=turned[:, :, 0])
+            return col
+
+        x_picked = keep.tile([P, PACK * R], BF16, name="x_picked")
+        xt_bf = keep.tile([P, G * D * PACK], BF16, name="xt_bf", align_bytes=64)
+        w_picked = keep.tile([P, PACK, N], F32, name="w_picked", tag="w_picked")
+        us_rows, c_tiles, x_bf, w_bf = {}, {}, {}, {}
+        x_codes, x_scales, xt_codes, xt_scales, w_codes, w_scales = {}, {}, {}, {}, {}, {}
+
+        def spread_us(g):
+            us_rows[g] = psum.tile([P, PACK, P], F32, name="us_rows", tag="dv_bank")
+            for t in range(PACK):
+                nc.tensor.transpose(us_rows[g][:, t, :], us_col[:, g, t:t + 1].to_broadcast([P, P]), ident[:])
+
+        def scale_table(b, g, c):
+            nc.scalar.activation(out=c.rearrange("p (u s e) -> p u s e", u=2, e=2),
+                                 in_=us_rows[g][:].rearrange("p (u e) s -> p u s e", e=2),
+                                 func=COPY, scale=ts_col[:, b:b + 1])
+            c_tiles[(b, g)] = c
+
+        def pick_users(j):
+            nc.vector.tensor_copy(x_picked[:, j * R:(j + 1) * R], u_win[j][:].indirect(users[:]))
+
+        def turn_users(j):
+            words = x_picked[:].bitcast(F32)[:, j * R // 2:(j + 1) * R // 2].rearrange("p (g s u) -> p g s u", g=G, u=2)
+            bank = psum.tile([P, G, 2, P], F32, name="xt_bank", tag="a_bank")
+            for g in range(G):
+                for u in range(2):
+                    nc.tensor.transpose(bank[:, g, u, :], words[:, g, :, u], ident[:])
+            nc.scalar.copy(out=xt_bf[:].bitcast(F32).rearrange("s (g j p u) -> s g j p u", g=G, j=PACK, u=2)[:, :, j],
+                           in_=bank[:].rearrange("s g u p -> s g p u"))
+
+        def weave_users(g):
+            x_bf[g] = keep.tile([P, PASS * PACK], BF16, name=f"x_bf{g}", align_bytes=64)
+            nc.scalar.copy(out=x_bf[g][:].rearrange("p (t s j) -> p s j t", t=PACK, j=PACK),
+                           in_=x_picked[:].rearrange("p (j g s t) -> p g s j t", j=PACK, g=G, t=PACK)[:, g])
+
+        def quantise(name, source, width, fmt):
+            codes = keep.tile([P, width], U32, name=f"{name}_codes", align_bytes=64)
+            scales = keep.tile([P, width], U8, name=f"{name}_scales", align_bytes=64)
+            nc.vector.quantize_mx(out=codes[:].bitcast(fmt), scales=scales[:], in_=source)
+            return codes, scales
+
+        def pick_items(j, lo, hi):
+            nc.vector.tensor_copy(w_picked[:, j, lo:hi], v_win[j][:].indirect(items[:, lo // 16:hi // 16]))
+
+        def weave_items(h):
+            w_bf[h] = keep.tile([P, HALF * PACK], BF16, name=f"w_bf{h}", align_bytes=64)
+            nc.scalar.copy(out=w_bf[h][:].rearrange("p (c i j) -> p c j i", i=4, j=PACK),
+                           in_=w_picked[:, :, h * HALF:(h + 1) * HALF].rearrange("p j (c i) -> p c j i", i=4))
+
+        u0_bf = keep.tile([P, TU], BF16, name="u0_bf")
+        nc.scalar.activation(out=u0_bf[:], in_=u_win[0][:], func=COPY)
+        ts_col = column_of("ts", ts_win)
+        nc.scalar.activation(out=x_picked[:, :R], in_=u0_bf[:].indirect(users[:]), func=COPY)
+        spread_us(0)
+        spread_us(1)
+        pick_users(1)
+        kb_col = column_of("kb", kb_win)
+        turn_users(1)
+        turn_users(0)
+        pick_users(2)
+        c_first = keep.tile([P, 2 * G * PASS], F32, name="c_first")
+        for g in range(G):
+            for b in range(2):
+                scale_table(b, g, c_first[:, (2 * g + b) * PASS:(2 * g + b + 1) * PASS])
+            if g == 0:
+                turn_users(2)
+        pick_users(3)
+        weave_users(0)
+        turn_users(3)
+        weave_users(1)
+        pick_items(0, 0, N)
+        pick_items(1, 0, N)
+        x_codes[0], x_scales[0] = quantise("x0", x_bf[0][:], PASS, E4M3)
+        pick_items(2, 0, N)
+        xt_codes[0], xt_scales[0] = quantise("xt0", xt_bf[:, :D * PACK], D, E4M3)
+        pick_items(3, 0, HALF)
+        weave_items(0)
+        pick_items(3, HALF, N)
+        weave_items(1)
+        x_codes[1], x_scales[1] = quantise("x1", x_bf[1][:], PASS, E4M3)
+        w_codes[0], w_scales[0] = quantise("w0", w_bf[0][:], HALF, E4M3)
+        xt_codes[1], xt_scales[1] = quantise("xt1", xt_bf[:, D * PACK:], D, E4M3)
+        c_second = keep.tile([P, 2 * G * PASS], F32, name="c_second", tag="w_picked")
+        for g in range(G):
+            for b in range(2):
+                scale_table(2 + b, g, c_second[:, (2 * g + b) * PASS:(2 * g + b + 1) * PASS])
+
+        h_codes = [keep.tile([P, N], U32, name=f"h_codes{g}", align_bytes=64) for g in range(G)]
+        h_scales = [keep.tile([P, N], U8, name=f"h_scales{g}", align_bytes=64) for g in range(G)]
+        for g in range(G):
+            nc.gpsimd.memset(h_codes[g][:, HALF:], 0)
+            nc.gpsimd.memset(h_scales[g][:, HALF:], 0)
+
+        def perm(bank):
+            return bank[:].rearrange("p (u e s) -> p u s e", u=2, e=2)
+
+        def split(tile):
+            return tile.rearrange("p (u s e) -> p u s e", u=2, e=2)
+
+        steps = [(h, g) for h in range(2) for g in range(G)]
+        y_banks, a_banks, scaled, resid, hq = {}, {}, {}, {}, {}
+
+        def turn_targets(n):
+            h, g = steps[n]
+            for k in range(2):
+                yb = psum.tile([P, PASS], F32, name="y_bank", tag="y_bank")
+                for t in range(PACK):
+                    nc.tensor.transpose(yb[:, t * P:(t + 1) * P], y_sb[(h, g)][:, t, k * P:(k + 1) * P], ident[:])
+                y_banks[(n, k)] = yb
+
+        def scores(n):
+            h, g = steps[n]
+            for k in range(2):
+                ab = psum.tile([P, PASS], F32, name="a_bank", tag="a_bank")
+                cols_k = slice(k * P, (k + 1) * P)
+                nc.tensor.matmul_mx(out=ab[:], lhsT=w_codes[h][:, cols_k].bitcast(E4M3), lhsT_scale=w_scales[h][:, cols_k],
+                                    rhs=x_codes[g][:].bitcast(E4M3), rhs_scale=x_scales[g][:], start=True, stop=True)
+                a_banks[(n, k)] = ab
+
+        def scale_scores(n):
+            h, g = steps[n]
+            for k in range(2):
+                sc = work.tile([P, PASS], F32, name="scaled")
+                nc.vector.tensor_tensor(split(sc[:]), perm(a_banks[(n, k)]), split(c_tiles[(2 * h + k, g)]), ALU.mult)
+                scaled[(n, k)] = sc
+
+        def residuals(n):
+            h, g = steps[n]
+            for k in range(2):
+                b = 2 * h + k
+                rs = work.tile([P, PASS], F32, name="resid", bufs=4)
+                for u in range(2):
+                    nc.vector.scalar_tensor_tensor(split(rs[:])[:, u], split(scaled[(n, k)][:])[:, u], kb_col[:, b:b + 1],
+                                                   perm(y_banks[(n, k)])[:, u], ALU.add, ALU.subtract)
+                resid[(n, k)] = rs
+
+        def weigh_and_turn(n, k, engine):
+            h, g = steps[n]
+            if k == 0:
+                hq[n] = work.tile([P, HALF * PACK], BF16, name="hq", align_bytes=64, bufs=4)
+            gr = work.tile([P, PASS], BF16, name="grad", align_bytes=64)
+            engine.tensor_tensor(gr[:], resid[(n, k)][:], c_tiles[(2 * h + k, g)], ALU.mult)
+            hb = psum.tile([P, 2, P], F32, name="h_bank", tag="h_bank")
+            gw = gr[:].bitcast(F32)
+            for u in range(2):
+                nc.tensor.transpose(hb[:, u, :], gw[:, u * P:(u + 1) * P], ident[:])
+            nc.scalar.copy(out=hq[n][:].bitcast(F32)[:, k * 2 * P:(k + 1) * 2 * P].rearrange("s (i u) -> s i u", u=2),
+                           in_=hb[:].rearrange("s u i -> s i u"))
+
+        def quantise_h(n):
+            h, g = steps[n]
+            cols_h = slice(h * HALF, (h + 1) * HALF)
+            nc.vector.quantize_mx(out=h_codes[g][:, cols_h].bitcast(E5M2), scales=h_scales[g][:, cols_h], in_=hq[n][:])
+
+        def gradient(j, lo, hi, tag):
+            dv = psum.tile([P, N], F32, name="dv_bank", tag=tag)
+            for g in range(G):
+                nc.tensor.matmul_mx(out=dv[:], lhsT=xt_codes[g][:, j * P:(j + 1) * P].bitcast(E4M3),
+                                    lhsT_scale=xt_scales[g][:, j * P:(j + 1) * P],
+                                    rhs=h_codes[g][:].bitcast(E5M2), rhs_scale=h_scales[g][:], start=(g == 0), stop=(g == G - 1))
+            dv_sb = keep.tile([P, hi - lo], F32, name=f"dv_sb{j}_{lo}")
+            nc.scalar.copy(out=dv_sb[:], in_=dv[:, lo:hi])
+            return dv_sb
+
+        def put(j, lo, hi, dv_sb):
+            nc.vector.tensor_copy(out_win[j][:].indirect(items[:, lo // 16:hi // 16]), dv_sb[:])
+
+        out_planes = out.rearrange("(p j) c -> j p c", j=PACK)
+        last = len(steps) - 1
+        turn_targets(0)
+        scores(0)
+        early = []
+        for n in range(len(steps)):
+            scale_scores(n)
+            if n == 0:
+                w_codes[1], w_scales[1] = quantise("w1", w_bf[1][:], HALF, E4M3)
+            if n < last:
+                scores(n + 1)
+            if n > 0:
+                weigh_and_turn(n - 1, 1, nc.gpsimd)
+            if n > 1:
+                quantise_h(n - 2)
+            if n == last:
+                early = [gradient(j, 0, HALF, "dv_bank") for j in range(2)]
+            residuals(n)
+            if n < last:
+                turn_targets(n + 1)
+            weigh_and_turn(n, 0, nc.gpsimd)
+        weigh_and_turn(last, 1, nc.vector)
+        put(0, 0, HALF, early[0])
+        quantise_h(last - 1)
+        quantise_h(last)
+        put(1, 0, HALF, early[1])
+        for j in range(PACK):
+            lo = HALF if j < 2 else 0
+            put(j, lo, N, gradient(j, lo, N, "dv_bank" if j < 2 else "a_bank"))
+            nc.sync.dma_start(out=out_planes[j], in_=out_win[j][:])

@@ -34,9 +34,8 @@ def tile_attend_gmf_sq_v_kb_kernel(tc, uT, vT, y, us, ts, kb, offs, uoffs, out):
 
         ts_win = keep.tile([P, T], F32, name="ts_win")
         kb_win = keep.tile([P, T], F32, name="kb_win")
-        nc.gpsimd.memset(ts_win[:, :T // 2], 0.0)
-        nc.vector.memset(ts_win[:, T // 2:], 0.0)
-        nc.vector.memset(kb_win[:], 0.0)
+        nc.vector.memset(ts_win[:].bitcast(U32), 0)
+        nc.vector.memset(kb_win[:].bitcast(U32), 0)
         ident = keep.tile([P, P], F32, name="ident")
         make_identity(nc, ident[:])
 
@@ -45,7 +44,7 @@ def tile_attend_gmf_sq_v_kb_kernel(tc, uT, vT, y, us, ts, kb, offs, uoffs, out):
         us_col = keep.tile([P, G, PACK], F32, name="us_col")
         u_planes = uT.rearrange("(p j) c -> j p c", j=PACK)
         v_planes = vT.rearrange("(p j) c -> j p c", j=PACK)
-        u_win = [keep.tile([P, TU], F32, name=f"u_win{j}") for j in range(PACK)]
+        u_win = [keep.tile([P, TU], F32, name=f"u_win{j}", tag=f"u_win{j}") for j in range(PACK)]
         v_win = [keep.tile([P, T], F32, name=f"v_win{j}") for j in range(PACK)]
         nc.sync.dma_start(out=u_win[0][:], in_=u_planes[0])
         nc.sync.dma_start(users[:], uoffs)
@@ -65,9 +64,10 @@ def tile_attend_gmf_sq_v_kb_kernel(tc, uT, vT, y, us, ts, kb, offs, uoffs, out):
                 nc.sync.dma_start(out=y_sb[(h, g)][:],
                                   in_=y[0, g * PASS:(g + 1) * PASS, h * HALF:(h + 1) * HALF].rearrange("(s t) i -> s t i", t=PACK))
 
-        out_win = [keep.tile([P, T], F32, name=f"out_win{j}") for j in range(PACK)]
-        for j in range(PACK):
-            nc.gpsimd.memset(out_win[j][:], 0.0)
+        out_win = {}
+        for j in range(2):
+            out_win[j] = keep.tile([P, T], F32, name=f"out_win{j}")
+            nc.vector.memset(out_win[j][:].bitcast(U32), 0)
 
         def column_of(name, win):
             picked = keep.tile([P, N], F32, name=f"{name}_picked")
@@ -110,8 +110,8 @@ def tile_attend_gmf_sq_v_kb_kernel(tc, uT, vT, y, us, ts, kb, offs, uoffs, out):
 
         def weave_users(g):
             x_bf[g] = keep.tile([P, PASS * PACK], BF16, name=f"x_bf{g}", align_bytes=64)
-            nc.scalar.copy(out=x_bf[g][:].rearrange("p (t s j) -> p s j t", t=PACK, j=PACK),
-                           in_=x_picked[:].rearrange("p (j g s t) -> p g s j t", j=PACK, g=G, t=PACK)[:, g])
+            nc.scalar.copy(out=x_bf[g][:].rearrange("p (c i j) -> p c j i", i=4, j=PACK),
+                           in_=x_picked[:].rearrange("p (j g c i) -> p g c j i", j=PACK, g=G, i=4)[:, g])
 
         def quantise(name, source, width, fmt):
             codes = keep.tile([P, width], U32, name=f"{name}_codes", align_bytes=64)
@@ -135,6 +135,9 @@ def tile_attend_gmf_sq_v_kb_kernel(tc, uT, vT, y, us, ts, kb, offs, uoffs, out):
         spread_us(1)
         pick_users(1)
         kb_col = column_of("kb", kb_win)
+        for j in range(2, PACK):
+            out_win[j] = keep.tile([P, T], F32, name=f"out_win{j}", tag=f"u_win{j - 2}")
+            nc.gpsimd.memset(out_win[j][:], 0.0)
         turn_users(1)
         turn_users(0)
         pick_users(2)
@@ -168,8 +171,8 @@ def tile_attend_gmf_sq_v_kb_kernel(tc, uT, vT, y, us, ts, kb, offs, uoffs, out):
         h_codes = [keep.tile([P, N], U32, name=f"h_codes{g}", align_bytes=64) for g in range(G)]
         h_scales = [keep.tile([P, N], U8, name=f"h_scales{g}", align_bytes=64) for g in range(G)]
         for g in range(G):
-            nc.gpsimd.memset(h_codes[g][:, HALF:], 0)
-            nc.gpsimd.memset(h_scales[g][:, HALF:], 0)
+            nc.vector.memset(h_codes[g][:, HALF:], 0)
+            nc.vector.memset(h_scales[g][:].bitcast(U32)[:, HALF // 4:], 0)
 
         def perm(bank):
             return bank[:].rearrange("p (u e s) -> p u s e", u=2, e=2)
@@ -201,18 +204,16 @@ def tile_attend_gmf_sq_v_kb_kernel(tc, uT, vT, y, us, ts, kb, offs, uoffs, out):
             h, g = steps[n]
             for k in range(2):
                 sc = work.tile([P, PASS], F32, name="scaled")
-                nc.vector.tensor_tensor(split(sc[:]), perm(a_banks[(n, k)]), split(c_tiles[(2 * h + k, g)]), ALU.mult)
+                nc.vector.tensor_tensor(split(sc[:]), a_banks[(n, k)][:].rearrange("p (s u e) -> p u s e", u=2, e=2), split(c_tiles[(2 * h + k, g)]), ALU.mult)
                 scaled[(n, k)] = sc
 
-        def residuals(n):
-            h, g = steps[n]
-            for k in range(2):
-                b = 2 * h + k
-                rs = work.tile([P, PASS], F32, name="resid", bufs=4)
-                for u in range(2):
-                    nc.vector.scalar_tensor_tensor(split(rs[:])[:, u], split(scaled[(n, k)][:])[:, u], kb_col[:, b:b + 1],
-                                                   perm(y_banks[(n, k)])[:, u], ALU.add, ALU.subtract)
-                resid[(n, k)] = rs
+        def residual(n, k):
+            b = 2 * steps[n][0] + k
+            rs = work.tile([P, PASS], F32, name="resid", bufs=4)
+            for u in range(2):
+                nc.vector.scalar_tensor_tensor(split(rs[:])[:, u], split(scaled[(n, k)][:])[:, u], kb_col[:, b:b + 1],
+                                               perm(y_banks[(n, k)])[:, u], ALU.add, ALU.subtract)
+            resid[(n, k)] = rs
 
         def weigh_and_turn(n, k, engine):
             h, g = steps[n]
@@ -258,15 +259,17 @@ def tile_attend_gmf_sq_v_kb_kernel(tc, uT, vT, y, us, ts, kb, offs, uoffs, out):
                 scores(n + 1)
             if n > 0:
                 weigh_and_turn(n - 1, 1, nc.gpsimd)
+            residual(n, 0)
             if n > 1:
                 quantise_h(n - 2)
             if n == last:
                 early = [gradient(j, 0, HALF, "dv_bank") for j in range(2)]
-            residuals(n)
+            residual(n, 1)
             if n < last:
                 turn_targets(n + 1)
-            weigh_and_turn(n, 0, nc.gpsimd)
-        weigh_and_turn(last, 1, nc.vector)
+                weigh_and_turn(n, 0, nc.gpsimd)
+        for k in range(2):
+            weigh_and_turn(last, k, nc.vector)
         put(0, 0, HALF, early[0])
         quantise_h(last - 1)
         quantise_h(last)

@@ -34,8 +34,9 @@ def tile_attend_gmf_sq_v_kb_kernel(tc, uT, vT, y, us, ts, kb, offs, uoffs, out):
 
         ts_win = keep.tile([P, T], F32, name="ts_win")
         kb_win = keep.tile([P, T], F32, name="kb_win")
-        nc.vector.memset(ts_win[:].bitcast(U32), 0)
-        nc.vector.memset(kb_win[:].bitcast(U32), 0)
+        for win in (ts_win, kb_win):
+            nc.gpsimd.memset(win[:, :T // 2], 0.0)
+            nc.vector.memset(win[:, T // 2:], 0.0)
         ident = keep.tile([P, P], F32, name="ident")
         make_identity(nc, ident[:])
 
@@ -45,7 +46,7 @@ def tile_attend_gmf_sq_v_kb_kernel(tc, uT, vT, y, us, ts, kb, offs, uoffs, out):
         u_planes = uT.rearrange("(p j) c -> j p c", j=PACK)
         v_planes = vT.rearrange("(p j) c -> j p c", j=PACK)
         u_win = [keep.tile([P, TU], F32, name=f"u_win{j}", tag=f"u_win{j}") for j in range(PACK)]
-        v_win = [keep.tile([P, T], F32, name=f"v_win{j}") for j in range(PACK)]
+        v_win = [keep.tile([P, T], F32, name=f"v_win{j}", tag=f"v_win{j}", align_bytes=64) for j in range(PACK)]
         nc.sync.dma_start(out=u_win[0][:], in_=u_planes[0])
         nc.sync.dma_start(users[:], uoffs)
         nc.sync.dma_start(items[:], offs)
@@ -64,10 +65,6 @@ def tile_attend_gmf_sq_v_kb_kernel(tc, uT, vT, y, us, ts, kb, offs, uoffs, out):
                 nc.sync.dma_start(out=y_sb[(h, g)][:],
                                   in_=y[0, g * PASS:(g + 1) * PASS, h * HALF:(h + 1) * HALF].rearrange("(s t) i -> s t i", t=PACK))
 
-        out_win = {}
-        for j in range(2):
-            out_win[j] = keep.tile([P, T], F32, name=f"out_win{j}")
-            nc.vector.memset(out_win[j][:].bitcast(U32), 0)
 
         def column_of(name, win):
             picked = keep.tile([P, N], F32, name=f"{name}_picked")
@@ -81,9 +78,9 @@ def tile_attend_gmf_sq_v_kb_kernel(tc, uT, vT, y, us, ts, kb, offs, uoffs, out):
 
         x_picked = keep.tile([P, PACK * R], BF16, name="x_picked")
         xt_bf = keep.tile([P, G * D * PACK], BF16, name="xt_bf", align_bytes=64)
-        w_picked = keep.tile([P, PACK, N], F32, name="w_picked", tag="w_picked")
+        w_picked = keep.tile([P, PACK * N], BF16, name="w_picked", tag="w_picked")
         us_rows, c_tiles, x_bf, w_bf = {}, {}, {}, {}
-        x_codes, x_scales, xt_codes, xt_scales, w_codes, w_scales = {}, {}, {}, {}, {}, {}
+        x_codes, x_scales, w_codes, w_scales = {}, {}, {}, {}
 
         def spread_us(g):
             us_rows[g] = psum.tile([P, PACK, P], F32, name="us_rows", tag="dv_bank")
@@ -113,19 +110,20 @@ def tile_attend_gmf_sq_v_kb_kernel(tc, uT, vT, y, us, ts, kb, offs, uoffs, out):
             nc.scalar.copy(out=x_bf[g][:].rearrange("p (c i j) -> p c j i", i=4, j=PACK),
                            in_=x_picked[:].rearrange("p (j g c i) -> p g c j i", j=PACK, g=G, i=4)[:, g])
 
-        def quantise(name, source, width, fmt):
-            codes = keep.tile([P, width], U32, name=f"{name}_codes", align_bytes=64)
+        def quantise(name, source, width, tag):
+            codes = keep.tile([P, width], U32, name=f"{name}_codes", tag=tag, align_bytes=64)
             scales = keep.tile([P, width], U8, name=f"{name}_scales", align_bytes=64)
-            nc.vector.quantize_mx(out=codes[:].bitcast(fmt), scales=scales[:], in_=source)
+            nc.vector.quantize_mx(out=codes[:].bitcast(E4M3), scales=scales[:], in_=source)
             return codes, scales
 
         def pick_items(j, lo, hi):
-            nc.vector.tensor_copy(w_picked[:, j, lo:hi], v_win[j][:].indirect(items[:, lo // 16:hi // 16]))
+            blocks = w_picked[:].rearrange("p (b j i) -> p j b i", b=NB, j=PACK)[:, j, lo // P:hi // P]
+            nc.vector.tensor_copy(blocks, v_win[j][:].indirect(items[:, lo // 16:hi // 16]))
 
-        def weave_items(h):
-            w_bf[h] = keep.tile([P, HALF * PACK], BF16, name=f"w_bf{h}", align_bytes=64)
-            nc.scalar.copy(out=w_bf[h][:].rearrange("p (c i j) -> p c j i", i=4, j=PACK),
-                           in_=w_picked[:, :, h * HALF:(h + 1) * HALF].rearrange("p j (c i) -> p c j i", i=4))
+        def weave_items(b):
+            w_bf[b] = keep.tile([P, PASS], BF16, name=f"w_bf{b}", tag=f"w_bf{b}", align_bytes=64)
+            nc.scalar.copy(out=w_bf[b][:].rearrange("p (c i j) -> p c j i", i=4, j=PACK),
+                           in_=w_picked[:, b * PASS:(b + 1) * PASS].rearrange("p (j c i) -> p c j i", j=PACK, i=4))
 
         u0_bf = keep.tile([P, TU], BF16, name="u0_bf")
         nc.scalar.activation(out=u0_bf[:], in_=u_win[0][:], func=COPY)
@@ -133,11 +131,14 @@ def tile_attend_gmf_sq_v_kb_kernel(tc, uT, vT, y, us, ts, kb, offs, uoffs, out):
         nc.scalar.activation(out=x_picked[:, :R], in_=u0_bf[:].indirect(users[:]), func=COPY)
         spread_us(0)
         spread_us(1)
+        out_win = [keep.tile([P, T], F32, name="out_win0")]
+        nc.vector.memset(out_win[0][:], 0.0)
         pick_users(1)
         kb_col = column_of("kb", kb_win)
-        for j in range(2, PACK):
-            out_win[j] = keep.tile([P, T], F32, name=f"out_win{j}", tag=f"u_win{j - 2}")
+        for j in range(1, 3):
+            out_win.append(keep.tile([P, T], F32, name=f"out_win{j}", tag=f"u_win{j - 1}"))
             nc.gpsimd.memset(out_win[j][:], 0.0)
+        out_win.append(out_win[0])
         turn_users(1)
         turn_users(0)
         pick_users(2)
@@ -153,16 +154,18 @@ def tile_attend_gmf_sq_v_kb_kernel(tc, uT, vT, y, us, ts, kb, offs, uoffs, out):
         weave_users(1)
         pick_items(0, 0, N)
         pick_items(1, 0, N)
-        x_codes[0], x_scales[0] = quantise("x0", x_bf[0][:], PASS, E4M3)
+        x_codes[0], x_scales[0] = quantise("x0", x_bf[0][:], PASS, "v_win1")
         pick_items(2, 0, N)
-        xt_codes[0], xt_scales[0] = quantise("xt0", xt_bf[:, :D * PACK], D, E4M3)
-        pick_items(3, 0, HALF)
-        weave_items(0)
+        xt_codes, xt_scales = quantise("xt", xt_bf[:], G * D, "v_win2")
+        for b in range(2):
+            pick_items(3, b * P, (b + 1) * P)
+            weave_items(b)
         pick_items(3, HALF, N)
-        weave_items(1)
-        x_codes[1], x_scales[1] = quantise("x1", x_bf[1][:], PASS, E4M3)
-        w_codes[0], w_scales[0] = quantise("w0", w_bf[0][:], HALF, E4M3)
-        xt_codes[1], xt_scales[1] = quantise("xt1", xt_bf[:, D * PACK:], D, E4M3)
+        weave_items(2)
+        weave_items(3)
+        w_codes[0], w_scales[0] = quantise("w0", w_bf[0][:], P, "w0_codes")
+        x_codes[1], x_scales[1] = quantise("x1", x_bf[1][:], PASS, "w_bf0")
+        w_codes[1], w_scales[1] = quantise("w1", w_bf[1][:], P, "w1_codes")
         c_second = keep.tile([P, 2 * G * PASS], F32, name="c_second", tag="w_picked")
         for g in range(G):
             for b in range(2):
@@ -195,8 +198,7 @@ def tile_attend_gmf_sq_v_kb_kernel(tc, uT, vT, y, us, ts, kb, offs, uoffs, out):
             h, g = steps[n]
             for k in range(2):
                 ab = psum.tile([P, PASS], F32, name="a_bank", tag="a_bank")
-                cols_k = slice(k * P, (k + 1) * P)
-                nc.tensor.matmul_mx(out=ab[:], lhsT=w_codes[h][:, cols_k].bitcast(E4M3), lhsT_scale=w_scales[h][:, cols_k],
+                nc.tensor.matmul_mx(out=ab[:], lhsT=w_codes[2 * h + k][:].bitcast(E4M3), lhsT_scale=w_scales[2 * h + k][:],
                                     rhs=x_codes[g][:].bitcast(E4M3), rhs_scale=x_scales[g][:], start=True, stop=True)
                 a_banks[(n, k)] = ab
 
@@ -236,8 +238,8 @@ def tile_attend_gmf_sq_v_kb_kernel(tc, uT, vT, y, us, ts, kb, offs, uoffs, out):
         def gradient(j, lo, hi, tag):
             dv = psum.tile([P, N], F32, name="dv_bank", tag=tag)
             for g in range(G):
-                nc.tensor.matmul_mx(out=dv[:], lhsT=xt_codes[g][:, j * P:(j + 1) * P].bitcast(E4M3),
-                                    lhsT_scale=xt_scales[g][:, j * P:(j + 1) * P],
+                nc.tensor.matmul_mx(out=dv[:], lhsT=xt_codes[:, g * D + j * P:g * D + (j + 1) * P].bitcast(E4M3),
+                                    lhsT_scale=xt_scales[:, g * D + j * P:g * D + (j + 1) * P],
                                     rhs=h_codes[g][:].bitcast(E5M2), rhs_scale=h_scales[g][:], start=(g == 0), stop=(g == G - 1))
             dv_sb = keep.tile([P, hi - lo], F32, name=f"dv_sb{j}_{lo}")
             nc.scalar.copy(out=dv_sb[:], in_=dv[:, lo:hi])
@@ -254,7 +256,8 @@ def tile_attend_gmf_sq_v_kb_kernel(tc, uT, vT, y, us, ts, kb, offs, uoffs, out):
         for n in range(len(steps)):
             scale_scores(n)
             if n == 0:
-                w_codes[1], w_scales[1] = quantise("w1", w_bf[1][:], HALF, E4M3)
+                for b in range(2, NB):
+                    w_codes[b], w_scales[b] = quantise(f"w{b}", w_bf[b][:], P, f"w{b}_codes")
             if n < last:
                 scores(n + 1)
             if n > 0:

@@ -10,6 +10,8 @@ PASS = P * PACK
 G = R // PASS
 NB = N // P
 HALF = N // 2
+RUN = 4
+PER_COLUMN = 16
 
 FLOPS = 2 * 2 * R * N * D
 BYTES = 4 * (D * TU + D * T + R * N + R + 2 * T + D * T) + 2 * P * (N + R) // 16
@@ -23,30 +25,33 @@ E4M3 = mybir.dt.float8_e4m3fn_x4
 E5M2 = mybir.dt.float8_e5m2_x4
 ALU = mybir.AluOpType
 COPY = mybir.ActivationFunctionType.Copy
+IDENTITY = mybir.ActivationFunctionType.Identity
 
 
 def tile_attend_gmf_sq_v_kb_kernel(tc, uT, vT, y, us, ts, kb, offs, uoffs, out):
     nc = tc.nc
     with ExitStack() as ctx:
         keep = ctx.enter_context(tc.tile_pool(name="keep", bufs=1))
-        work = ctx.enter_context(tc.tile_pool(name="work", bufs=2))
+        work = ctx.enter_context(tc.tile_pool(name="work", bufs=3))
         psum = ctx.enter_context(tc.psum_pool(name="psum", bufs=2))
 
         ts_win = keep.tile([P, T], F32, name="ts_win")
         kb_win = keep.tile([P, T], F32, name="kb_win")
+        out_win = [keep.tile([P, T], F32, name="out_win0")]
         for win in (ts_win, kb_win):
             nc.gpsimd.memset(win[:, :T // 2], 0.0)
             nc.vector.memset(win[:, T // 2:], 0.0)
+        nc.vector.memset(out_win[0][:], 0.0)
         ident = keep.tile([P, P], F32, name="ident")
         make_identity(nc, ident[:])
 
-        items = keep.tile([P, N // 16], U16, name="items")
-        users = keep.tile([P, R // 16], U16, name="users")
+        items = keep.tile([P, N // PER_COLUMN], U16, name="items")
+        users = keep.tile([P, R // PER_COLUMN], U16, name="users")
         us_col = keep.tile([P, G, PACK], F32, name="us_col")
         u_planes = uT.rearrange("(p j) c -> j p c", j=PACK)
         v_planes = vT.rearrange("(p j) c -> j p c", j=PACK)
         u_win = [keep.tile([P, TU], F32, name=f"u_win{j}", tag=f"u_win{j}") for j in range(PACK)]
-        v_win = [keep.tile([P, T], F32, name=f"v_win{j}", tag=f"v_win{j}", align_bytes=64) for j in range(PACK)]
+        v_win = [keep.tile([P, T], F32, name=f"v_win{j}") for j in range(PACK)]
         nc.sync.dma_start(out=u_win[0][:], in_=u_planes[0])
         nc.sync.dma_start(users[:], uoffs)
         nc.sync.dma_start(items[:], offs)
@@ -65,36 +70,46 @@ def tile_attend_gmf_sq_v_kb_kernel(tc, uT, vT, y, us, ts, kb, offs, uoffs, out):
                 nc.sync.dma_start(out=y_sb[(h, g)][:],
                                   in_=y[0, g * PASS:(g + 1) * PASS, h * HALF:(h + 1) * HALF].rearrange("(s t) i -> s t i", t=PACK))
 
+        def gather(on_scalar, dst, win, offsets):
+            if on_scalar:
+                nc.scalar.activation(out=dst, in_=win[:].indirect(offsets), func=COPY)
+            else:
+                nc.vector.tensor_copy(dst, win[:].indirect(offsets))
 
-        def column_of(name, win):
+        def scatter(on_scalar, win, offsets, src):
+            if on_scalar:
+                nc.scalar.activation(out=win[:].indirect(offsets), in_=src, func=COPY)
+            else:
+                nc.vector.tensor_copy(win[:].indirect(offsets), src)
+
+        def slots(lo, hi):
+            return items[:, lo // PER_COLUMN:hi // PER_COLUMN]
+
+        def negated_column(name, win, on_scalar):
             picked = keep.tile([P, N], F32, name=f"{name}_picked")
-            nc.vector.tensor_copy(picked[:], win[:].indirect(items[:]))
-            turned = psum.tile([P, NB, P], F32, name="turned", tag="h_bank")
+            gather(on_scalar, picked[:], win, items[:])
+            turned = psum.tile([P, NB, P], F32, name="turned", tag="y_bank")
             for b in range(NB):
                 nc.tensor.transpose(turned[:, b, :], picked[:, b * P:(b + 1) * P], ident[:])
-            col = keep.tile([P, NB], F32, name=f"{name}_col")
-            nc.scalar.copy(out=col[:], in_=turned[:, :, 0])
+            col = keep.tile([P, NB], F32, name=f"neg_{name}")
+            nc.scalar.activation(out=col[:], in_=turned[:, :, 0], func=COPY, scale=-1.0)
             return col
 
         x_picked = keep.tile([P, PACK * R], BF16, name="x_picked")
         xt_bf = keep.tile([P, G * D * PACK], BF16, name="xt_bf", align_bytes=64)
-        w_picked = keep.tile([P, PACK * N], BF16, name="w_picked", tag="w_picked")
-        us_rows, c_tiles, x_bf, w_bf = {}, {}, {}, {}
+        w_picked = keep.tile([P, PACK * N], BF16, name="w_picked")
+        us_rows, x_bf, w_bf = {}, {}, {}
         x_codes, x_scales, w_codes, w_scales = {}, {}, {}, {}
 
         def spread_us(g):
-            us_rows[g] = psum.tile([P, PACK, P], F32, name="us_rows", tag="dv_bank")
+            bank = psum.tile([P, PACK, P], F32, name="us_bank", tag="z_bank")
             for t in range(PACK):
-                nc.tensor.transpose(us_rows[g][:, t, :], us_col[:, g, t:t + 1].to_broadcast([P, P]), ident[:])
+                nc.tensor.transpose(bank[:, t, :], us_col[:, g, t:t + 1].to_broadcast([P, P]), ident[:])
+            us_rows[g] = keep.tile([P, PACK, P], F32, name=f"us_rows{g}")
+            nc.scalar.activation(out=us_rows[g][:], in_=bank[:], func=COPY)
 
-        def scale_table(b, g, c):
-            nc.scalar.activation(out=c.rearrange("p (u s e) -> p u s e", u=2, e=2),
-                                 in_=us_rows[g][:].rearrange("p (u e) s -> p u s e", e=2),
-                                 func=COPY, scale=ts_col[:, b:b + 1])
-            c_tiles[(b, g)] = c
-
-        def pick_users(j):
-            nc.vector.tensor_copy(x_picked[:, j * R:(j + 1) * R], u_win[j][:].indirect(users[:]))
+        def pick_users(j, on_scalar):
+            gather(on_scalar, x_picked[:, j * R:(j + 1) * R], u_win[j], users[:])
 
         def turn_users(j):
             words = x_picked[:].bitcast(F32)[:, j * R // 2:(j + 1) * R // 2].rearrange("p (g s u) -> p g s u", g=G, u=2)
@@ -105,179 +120,172 @@ def tile_attend_gmf_sq_v_kb_kernel(tc, uT, vT, y, us, ts, kb, offs, uoffs, out):
             nc.scalar.copy(out=xt_bf[:].bitcast(F32).rearrange("s (g j p u) -> s g j p u", g=G, j=PACK, u=2)[:, :, j],
                            in_=bank[:].rearrange("s g u p -> s g p u"))
 
-        def weave_users(g):
-            x_bf[g] = keep.tile([P, PASS * PACK], BF16, name=f"x_bf{g}", align_bytes=64)
-            nc.scalar.copy(out=x_bf[g][:].rearrange("p (c i j) -> p c j i", i=4, j=PACK),
-                           in_=x_picked[:].rearrange("p (j g c i) -> p g c j i", j=PACK, g=G, i=4)[:, g])
+        def weave(on_scalar, dst, src):
+            if on_scalar:
+                nc.scalar.copy(out=dst, in_=src)
+            else:
+                nc.vector.tensor_copy(dst, src)
 
-        def quantise(name, source, width, tag):
-            codes = keep.tile([P, width], U32, name=f"{name}_codes", tag=tag, align_bytes=64)
+        def weave_users(g, on_scalar):
+            x_bf[g] = keep.tile([P, PASS * PACK], BF16, name=f"x_bf{g}", align_bytes=64)
+            weave(on_scalar, x_bf[g][:].rearrange("p (c i j) -> p c j i", i=RUN, j=PACK),
+                  x_picked[:].rearrange("p (j g c i) -> p g c j i", j=PACK, g=G, i=RUN)[:, g])
+
+        def quantise(name, source, width):
+            codes = keep.tile([P, width], U32, name=f"{name}_codes", align_bytes=64)
             scales = keep.tile([P, width], U8, name=f"{name}_scales", align_bytes=64)
             nc.vector.quantize_mx(out=codes[:].bitcast(E4M3), scales=scales[:], in_=source)
             return codes, scales
 
-        def pick_items(j, lo, hi):
-            blocks = w_picked[:].rearrange("p (b j i) -> p j b i", b=NB, j=PACK)[:, j, lo // P:hi // P]
-            nc.vector.tensor_copy(blocks, v_win[j][:].indirect(items[:, lo // 16:hi // 16]))
+        def pick_items(j, b, on_scalar):
+            at = (b * PACK + j) * P
+            gather(on_scalar, w_picked[:, at:at + P], v_win[j], slots(b * P, (b + 1) * P))
 
-        def weave_items(b):
-            w_bf[b] = keep.tile([P, PASS], BF16, name=f"w_bf{b}", tag=f"w_bf{b}", align_bytes=64)
-            nc.scalar.copy(out=w_bf[b][:].rearrange("p (c i j) -> p c j i", i=4, j=PACK),
-                           in_=w_picked[:, b * PASS:(b + 1) * PASS].rearrange("p (j c i) -> p c j i", j=PACK, i=4))
+        def pick_item_plane(j):
+            blocks = w_picked[:].rearrange("p (b j i) -> p j b i", b=NB, j=PACK)[:, j]
+            gather(False, blocks, v_win[j], items[:])
 
-        u0_bf = keep.tile([P, TU], BF16, name="u0_bf")
-        nc.scalar.activation(out=u0_bf[:], in_=u_win[0][:], func=COPY)
-        ts_col = column_of("ts", ts_win)
-        nc.scalar.activation(out=x_picked[:, :R], in_=u0_bf[:].indirect(users[:]), func=COPY)
-        spread_us(0)
-        spread_us(1)
-        out_win = [keep.tile([P, T], F32, name="out_win0")]
-        nc.vector.memset(out_win[0][:], 0.0)
-        pick_users(1)
-        kb_col = column_of("kb", kb_win)
-        for j in range(1, 3):
+        def weave_items(b, on_scalar):
+            w_bf[b] = keep.tile([P, PASS], BF16, name=f"w_bf{b}", align_bytes=64)
+            weave(on_scalar, w_bf[b][:].rearrange("p (c i j) -> p c j i", i=RUN, j=PACK),
+                  w_picked[:, b * PASS:(b + 1) * PASS].rearrange("p (j c i) -> p c j i", j=PACK, i=RUN))
+
+        def clear_window(j):
             out_win.append(keep.tile([P, T], F32, name=f"out_win{j}", tag=f"u_win{j - 1}"))
             nc.gpsimd.memset(out_win[j][:], 0.0)
-        out_win.append(out_win[0])
-        turn_users(1)
+
+        spread_us(0)
+        spread_us(1)
+        neg_ts = negated_column("ts", ts_win, True)
+        pick_users(0, False)
+        clear_window(1)
+        pick_users(1, False)
+        clear_window(2)
+        neg_kb = negated_column("kb", kb_win, True)
+        ts_sq = keep.tile([P, NB], F32, name="ts_sq")
+        ts_kb = keep.tile([P, NB], F32, name="ts_kb")
+        nc.gpsimd.tensor_tensor(ts_sq[:], neg_ts[:], neg_ts[:], ALU.mult)
+        nc.gpsimd.tensor_tensor(ts_kb[:], neg_ts[:], neg_kb[:], ALU.mult)
+        pick_users(2, False)
+        clear_window(3)
         turn_users(0)
-        pick_users(2)
-        c_first = keep.tile([P, 2 * G * PASS], F32, name="c_first")
-        for g in range(G):
-            for b in range(2):
-                scale_table(b, g, c_first[:, (2 * g + b) * PASS:(2 * g + b + 1) * PASS])
-            if g == 0:
-                turn_users(2)
-        pick_users(3)
-        weave_users(0)
+        turn_users(1)
+        pick_users(3, True)
+        pick_item_plane(0)
+        weave_users(0, False)
+        turn_users(2)
         turn_users(3)
-        weave_users(1)
-        pick_items(0, 0, N)
-        pick_items(1, 0, N)
-        x_codes[0], x_scales[0] = quantise("x0", x_bf[0][:], PASS, "v_win1")
-        pick_items(2, 0, N)
-        xt_codes, xt_scales = quantise("xt", xt_bf[:], G * D, "v_win2")
+        for b in range(NB):
+            pick_items(1, b, True)
+        x_codes[0], x_scales[0] = quantise("x0", x_bf[0][:], PASS)
+        weave_users(1, True)
+        xt_codes, xt_scales = quantise("xt", xt_bf[:], G * D)
+        pick_item_plane(2)
+        x_codes[1], x_scales[1] = quantise("x1", x_bf[1][:], PASS)
+        pick_items(3, 0, False)
+        pick_items(3, 1, True)
+        weave_items(0, False)
+        weave_items(1, True)
         for b in range(2):
-            pick_items(3, b * P, (b + 1) * P)
-            weave_items(b)
-        pick_items(3, HALF, N)
-        weave_items(2)
-        weave_items(3)
-        w_codes[0], w_scales[0] = quantise("w0", w_bf[0][:], P, "w0_codes")
-        x_codes[1], x_scales[1] = quantise("x1", x_bf[1][:], PASS, "w_bf0")
-        w_codes[1], w_scales[1] = quantise("w1", w_bf[1][:], P, "w1_codes")
-        c_second = keep.tile([P, 2 * G * PASS], F32, name="c_second", tag="w_picked")
-        for g in range(G):
-            for b in range(2):
-                scale_table(2 + b, g, c_second[:, (2 * g + b) * PASS:(2 * g + b + 1) * PASS])
+            w_codes[b], w_scales[b] = quantise(f"w{b}", w_bf[b][:], P)
 
         h_codes = [keep.tile([P, N], U32, name=f"h_codes{g}", align_bytes=64) for g in range(G)]
         h_scales = [keep.tile([P, N], U8, name=f"h_scales{g}", align_bytes=64) for g in range(G)]
-        for g in range(G):
-            nc.vector.memset(h_codes[g][:, HALF:], 0)
-            nc.vector.memset(h_scales[g][:].bitcast(U32)[:, HALF // 4:], 0)
+        tiles = [(2 * h + k, g) for h in range(2) for g in range(G) for k in range(2)]
+        targets, a_banks, scaled, z_banks, h_bf = {}, {}, {}, {}, {}
 
-        def perm(bank):
-            return bank[:].rearrange("p (u e s) -> p u s e", u=2, e=2)
-
-        def split(tile):
-            return tile.rearrange("p (u s e) -> p u s e", u=2, e=2)
-
-        steps = [(h, g) for h in range(2) for g in range(G)]
-        y_banks, a_banks, scaled, resid, hq = {}, {}, {}, {}, {}
-
-        def turn_targets(n):
-            h, g = steps[n]
-            for k in range(2):
-                yb = psum.tile([P, PASS], F32, name="y_bank", tag="y_bank")
-                for t in range(PACK):
-                    nc.tensor.transpose(yb[:, t * P:(t + 1) * P], y_sb[(h, g)][:, t, k * P:(k + 1) * P], ident[:])
-                y_banks[(n, k)] = yb
+        def target_term(n):
+            b, g = tiles[n]
+            bank = psum.tile([P, PASS], F32, name="y_bank", tag="y_bank")
+            for t in range(PACK):
+                nc.tensor.transpose(bank[:, t * P:(t + 1) * P], y_sb[(b // 2, g)][:, t, (b % 2) * P:(b % 2 + 1) * P], ident[:])
+            targets[n] = work.tile([P, PASS], F32, name="target", bufs=4)
+            nc.scalar.activation(out=targets[n][:], in_=bank[:], func=IDENTITY, scale=neg_ts[:, b:b + 1], bias=ts_kb[:, b:b + 1])
 
         def scores(n):
-            h, g = steps[n]
-            for k in range(2):
-                ab = psum.tile([P, PASS], F32, name="a_bank", tag="a_bank")
-                nc.tensor.matmul_mx(out=ab[:], lhsT=w_codes[2 * h + k][:].bitcast(E4M3), lhsT_scale=w_scales[2 * h + k][:],
-                                    rhs=x_codes[g][:].bitcast(E4M3), rhs_scale=x_scales[g][:], start=True, stop=True)
-                a_banks[(n, k)] = ab
+            b, g = tiles[n]
+            a_banks[n] = psum.tile([P, PASS], F32, name="a_bank", tag="a_bank")
+            nc.tensor.matmul_mx(out=a_banks[n][:], lhsT=w_codes[b][:].bitcast(E4M3), lhsT_scale=w_scales[b][:],
+                                rhs=x_codes[g][:].bitcast(E4M3), rhs_scale=x_scales[g][:], start=True, stop=True)
 
-        def scale_scores(n):
-            h, g = steps[n]
-            for k in range(2):
-                sc = work.tile([P, PASS], F32, name="scaled")
-                nc.vector.tensor_tensor(split(sc[:]), a_banks[(n, k)][:].rearrange("p (s u e) -> p u s e", u=2, e=2), split(c_tiles[(2 * h + k, g)]), ALU.mult)
-                scaled[(n, k)] = sc
+        def score_term(n):
+            b, g = tiles[n]
+            scaled[n] = work.tile([P, PACK, P], F32, name="scaled", tag="scaled")
+            nc.vector.scalar_tensor_tensor(scaled[n][:], a_banks[n][:].rearrange("p (s t) -> p t s", t=PACK), ts_sq[:, b:b + 1],
+                                           us_rows[g][:], ALU.mult, ALU.mult)
 
-        def residual(n, k):
-            b = 2 * steps[n][0] + k
-            rs = work.tile([P, PASS], F32, name="resid", bufs=4)
-            for u in range(2):
-                nc.vector.scalar_tensor_tensor(split(rs[:])[:, u], split(scaled[(n, k)][:])[:, u], kb_col[:, b:b + 1],
-                                               perm(y_banks[(n, k)])[:, u], ALU.add, ALU.subtract)
-            resid[(n, k)] = rs
+        def add_terms(n):
+            z_banks[n] = psum.tile([P, PACK, P], F32, name="z_bank", tag="z_bank")
+            for t in range(PACK):
+                nc.tensor.matmul(z_banks[n][:, t, :], targets[n][:, t * P:(t + 1) * P], ident[:], start=(t == 0), stop=False, is_transpose=True)
+            for t in range(PACK):
+                nc.tensor.matmul(z_banks[n][:, t, :], scaled[n][:, t, :], ident[:], start=False, stop=(t == PACK - 1), is_transpose=True)
 
-        def weigh_and_turn(n, k, engine):
-            h, g = steps[n]
-            if k == 0:
-                hq[n] = work.tile([P, HALF * PACK], BF16, name="hq", align_bytes=64, bufs=4)
-            gr = work.tile([P, PASS], BF16, name="grad", align_bytes=64)
-            engine.tensor_tensor(gr[:], resid[(n, k)][:], c_tiles[(2 * h + k, g)], ALU.mult)
-            hb = psum.tile([P, 2, P], F32, name="h_bank", tag="h_bank")
-            gw = gr[:].bitcast(F32)
-            for u in range(2):
-                nc.tensor.transpose(hb[:, u, :], gw[:, u * P:(u + 1) * P], ident[:])
-            nc.scalar.copy(out=hq[n][:].bitcast(F32)[:, k * 2 * P:(k + 1) * 2 * P].rearrange("s (i u) -> s i u", u=2),
-                           in_=hb[:].rearrange("s u i -> s i u"))
+        def round_h(n):
+            b, g = tiles[n]
+            h_bf[n] = work.tile([P, P, PACK], BF16, name="h_bf", align_bytes=64)
+            nc.vector.tensor_tensor(h_bf[n][:], z_banks[n][:].rearrange("s t i -> s i t"),
+                                    us_col[:, g:g + 1, :].to_broadcast([P, P, PACK]), ALU.mult)
 
         def quantise_h(n):
-            h, g = steps[n]
-            cols_h = slice(h * HALF, (h + 1) * HALF)
-            nc.vector.quantize_mx(out=h_codes[g][:, cols_h].bitcast(E5M2), scales=h_scales[g][:, cols_h], in_=hq[n][:])
+            b, g = tiles[n]
+            cols = slice(b * P, (b + 1) * P)
+            nc.vector.quantize_mx(out=h_codes[g][:, cols].bitcast(E5M2), scales=h_scales[g][:, cols],
+                                  in_=h_bf[n][:].rearrange("s i t -> s (i t)"))
 
-        def gradient(j, lo, hi, tag):
-            dv = psum.tile([P, N], F32, name="dv_bank", tag=tag)
+        def gradient(j, lo, hi, bank):
             for g in range(G):
-                nc.tensor.matmul_mx(out=dv[:], lhsT=xt_codes[:, g * D + j * P:g * D + (j + 1) * P].bitcast(E4M3),
-                                    lhsT_scale=xt_scales[:, g * D + j * P:g * D + (j + 1) * P],
-                                    rhs=h_codes[g][:].bitcast(E5M2), rhs_scale=h_scales[g][:], start=(g == 0), stop=(g == G - 1))
-            dv_sb = keep.tile([P, hi - lo], F32, name=f"dv_sb{j}_{lo}")
-            nc.scalar.copy(out=dv_sb[:], in_=dv[:, lo:hi])
-            return dv_sb
-
-        def put(j, lo, hi, dv_sb):
-            nc.vector.tensor_copy(out_win[j][:].indirect(items[:, lo // 16:hi // 16]), dv_sb[:])
+                at = g * D + j * P
+                nc.tensor.matmul_mx(out=bank, lhsT=xt_codes[:, at:at + P].bitcast(E4M3), lhsT_scale=xt_scales[:, at:at + P],
+                                    rhs=h_codes[g][:, lo:hi].bitcast(E5M2), rhs_scale=h_scales[g][:, lo:hi],
+                                    start=(g == 0), stop=(g == G - 1))
 
         out_planes = out.rearrange("(p j) c -> j p c", j=PACK)
-        last = len(steps) - 1
-        turn_targets(0)
-        scores(0)
-        early = []
-        for n in range(len(steps)):
-            scale_scores(n)
-            if n == 0:
-                for b in range(2, NB):
-                    w_codes[b], w_scales[b] = quantise(f"w{b}", w_bf[b][:], P, f"w{b}_codes")
-            if n < last:
-                scores(n + 1)
-            if n > 0:
-                weigh_and_turn(n - 1, 1, nc.gpsimd)
-            residual(n, 0)
-            if n > 1:
-                quantise_h(n - 2)
-            if n == last:
-                early = [gradient(j, 0, HALF, "dv_bank") for j in range(2)]
-            residual(n, 1)
-            if n < last:
-                turn_targets(n + 1)
-                weigh_and_turn(n, 0, nc.gpsimd)
-        for k in range(2):
-            weigh_and_turn(last, k, nc.vector)
-        put(0, 0, HALF, early[0])
-        quantise_h(last - 1)
-        quantise_h(last)
-        put(1, 0, HALF, early[1])
+        count = len(tiles)
+        for n in range(2):
+            target_term(n)
+        for n in range(2):
+            scores(n)
+        for b in range(2, NB):
+            pick_items(3, b, True)
+            weave_items(b, True)
+        for n in range(count + 3):
+            if n < count:
+                score_term(n)
+            if n + 2 < count:
+                target_term(n + 2)
+                if n + 2 == count // 2:
+                    for b in range(2, NB):
+                        w_codes[b], w_scales[b] = quantise(f"w{b}", w_bf[b][:], P)
+                scores(n + 2)
+            if n < count:
+                add_terms(n)
+            if 0 <= n - 2 < count:
+                round_h(n - 2)
+            if 0 <= n - 3 < count:
+                quantise_h(n - 3)
+            if n - 3 == count // 2 - 1:
+                early = psum.tile([P, 2, HALF], F32, name="early", tag="d_bank")
+                for j in range(2):
+                    gradient(j, 0, HALF, early[:, j, :])
+                early0 = keep.tile([P, HALF], F32, name="early0")
+                nc.scalar.copy(out=early0[:], in_=early[:, 0, :])
+                scatter(True, out_win[0], slots(0, HALF), early0[:])
+            if n == count - 1:
+                early1 = work.tile([P, HALF], F32, name="early1", tag="scaled")
+                nc.scalar.copy(out=early1[:], in_=early[:, 1, :])
+
+        scatter(False, out_win[1], slots(0, HALF), early1[:])
         for j in range(PACK):
             lo = HALF if j < 2 else 0
-            put(j, lo, N, gradient(j, lo, N, "dv_bank" if j < 2 else "a_bank"))
+            bank = psum.tile([P, N - lo], F32, name="dv_bank", tag="y_bank" if j < 2 else "a_bank")
+            gradient(j, lo, N, bank[:])
+            staged = keep.tile([P, N - lo], F32, name=f"staged{j}")
+            on_scalar = j % 2 == 0
+            weave(on_scalar, staged[:], bank[:])
+            if j == 2:
+                for h in range(2):
+                    scatter(True, out_win[j], slots(h * HALF, (h + 1) * HALF), staged[:, h * HALF:(h + 1) * HALF])
+            else:
+                scatter(on_scalar, out_win[j], slots(lo, N), staged[:])
             nc.sync.dma_start(out=out_planes[j], in_=out_win[j][:])

@@ -12,6 +12,8 @@ NB = N // P
 HALF = N // 2
 RUN = 4
 PER_COLUMN = 16
+LIVE = P - 1
+KINDS = "ttttssss"
 
 FLOPS = 2 * 2 * R * N * D
 BYTES = 4 * (D * TU + D * T + R * N + R + 2 * T + D * T) + 2 * P * (N + R) // 16
@@ -35,30 +37,31 @@ def tile_attend_gmf_sq_v_kb_kernel(tc, uT, vT, y, us, ts, kb, offs, uoffs, out):
         work = ctx.enter_context(tc.tile_pool(name="work", bufs=3))
         psum = ctx.enter_context(tc.psum_pool(name="psum", bufs=2))
 
-        ts_win = keep.tile([P, T], F32, name="ts_win")
-        kb_win = keep.tile([P, T], F32, name="kb_win")
-        out_win = [keep.tile([P, T], F32, name="out_win0")]
-        for win in (ts_win, kb_win):
-            nc.gpsimd.memset(win[:, :T // 2], 0.0)
-            nc.vector.memset(win[:, T // 2:], 0.0)
-        nc.vector.memset(out_win[0][:], 0.0)
         ident = keep.tile([P, P], F32, name="ident")
         make_identity(nc, ident[:])
+        ts_win = keep.tile([P, T], F32, name="ts_win")
+        kb_win = keep.tile([P, T], F32, name="kb_win")
+        out_win = []
+        for win in (ts_win, kb_win):
+            nc.vector.memset(win[:LIVE, :], 0.0)
+        for j in range(PACK):
+            out_win.append(keep.tile([P, T], F32, name=f"out_win{j}"))
+            nc.gpsimd.memset(out_win[j][:], 0.0)
 
         items = keep.tile([P, N // PER_COLUMN], U16, name="items")
         users = keep.tile([P, R // PER_COLUMN], U16, name="users")
         us_col = keep.tile([P, G, PACK], F32, name="us_col")
         u_planes = uT.rearrange("(p j) c -> j p c", j=PACK)
         v_planes = vT.rearrange("(p j) c -> j p c", j=PACK)
-        u_win = [keep.tile([P, TU], F32, name=f"u_win{j}", tag=f"u_win{j}") for j in range(PACK)]
+        u_win = [keep.tile([P, TU], F32, name=f"u_win{j}", tag=f"u_win{j}", align_bytes=64) for j in range(PACK)]
         v_win = [keep.tile([P, T], F32, name=f"v_win{j}") for j in range(PACK)]
+        nc.scalar.dma_start(out=us_col[:], in_=us[0].rearrange("(g s t) o -> s g (t o)", g=G, t=PACK))
+        nc.scalar.dma_start(out=ts_win[LIVE:, :], in_=ts[0:1, :])
+        nc.scalar.dma_start(out=kb_win[LIVE:, :], in_=kb[0:1, :])
         nc.sync.dma_start(out=u_win[0][:], in_=u_planes[0])
         nc.sync.dma_start(users[:], uoffs)
         nc.sync.dma_start(items[:], offs)
-        nc.sync.dma_start(out=ts_win[0:1, :], in_=ts[0:1, :])
-        nc.sync.dma_start(out=us_col[:], in_=us[0].rearrange("(g s t) o -> s g (t o)", g=G, t=PACK))
         nc.sync.dma_start(out=u_win[1][:], in_=u_planes[1])
-        nc.sync.dma_start(out=kb_win[0:1, :], in_=kb[0:1, :])
         for j in range(2, PACK):
             nc.sync.dma_start(out=u_win[j][:], in_=u_planes[j])
         for j in range(PACK):
@@ -92,11 +95,10 @@ def tile_attend_gmf_sq_v_kb_kernel(tc, uT, vT, y, us, ts, kb, offs, uoffs, out):
             for b in range(NB):
                 nc.tensor.transpose(turned[:, b, :], picked[:, b * P:(b + 1) * P], ident[:])
             col = keep.tile([P, NB], F32, name=f"neg_{name}")
-            nc.scalar.activation(out=col[:], in_=turned[:, :, 0], func=COPY, scale=-1.0)
+            nc.scalar.activation(out=col[:], in_=turned[:, :, LIVE], func=COPY, scale=-1.0)
             return col
 
         x_picked = keep.tile([P, PACK * R], BF16, name="x_picked")
-        xt_bf = keep.tile([P, G * D * PACK], BF16, name="xt_bf", align_bytes=64)
         w_picked = keep.tile([P, PACK * N], BF16, name="w_picked")
         us_rows, x_bf, w_bf = {}, {}, {}
         x_codes, x_scales, w_codes, w_scales = {}, {}, {}, {}
@@ -108,27 +110,27 @@ def tile_attend_gmf_sq_v_kb_kernel(tc, uT, vT, y, us, ts, kb, offs, uoffs, out):
             us_rows[g] = keep.tile([P, PACK, P], F32, name=f"us_rows{g}")
             nc.scalar.activation(out=us_rows[g][:], in_=bank[:], func=COPY)
 
-        def pick_users(j, on_scalar):
-            gather(on_scalar, x_picked[:, j * R:(j + 1) * R], u_win[j], users[:])
+        def pick_users(j, lo, hi, on_scalar):
+            gather(on_scalar, x_picked[:, j * R + lo:j * R + hi], u_win[j], users[:, lo // PER_COLUMN:hi // PER_COLUMN])
+
+        def move(on_scalar, dst, src):
+            if on_scalar:
+                nc.scalar.copy(out=dst, in_=src)
+            else:
+                nc.vector.tensor_copy(dst, src)
 
         def turn_users(j):
             words = x_picked[:].bitcast(F32)[:, j * R // 2:(j + 1) * R // 2].rearrange("p (g s u) -> p g s u", g=G, u=2)
-            bank = psum.tile([P, G, 2, P], F32, name="xt_bank", tag="a_bank")
+            bank = psum.tile([P, G, 2, P], F32, name="xt_bank", tag="a_bank" if j < 2 else "y_bank")
             for g in range(G):
                 for u in range(2):
                     nc.tensor.transpose(bank[:, g, u, :], words[:, g, :, u], ident[:])
             nc.scalar.copy(out=xt_bf[:].bitcast(F32).rearrange("s (g j p u) -> s g j p u", g=G, j=PACK, u=2)[:, :, j],
                            in_=bank[:].rearrange("s g u p -> s g p u"))
 
-        def weave(on_scalar, dst, src):
-            if on_scalar:
-                nc.scalar.copy(out=dst, in_=src)
-            else:
-                nc.vector.tensor_copy(dst, src)
-
         def weave_users(g, on_scalar):
             x_bf[g] = keep.tile([P, PASS * PACK], BF16, name=f"x_bf{g}", align_bytes=64)
-            weave(on_scalar, x_bf[g][:].rearrange("p (c i j) -> p c j i", i=RUN, j=PACK),
+            move(on_scalar, x_bf[g][:].rearrange("p (c i j) -> p c j i", i=RUN, j=PACK),
                   x_picked[:].rearrange("p (j g c i) -> p g c j i", j=PACK, g=G, i=RUN)[:, g])
 
         def quantise(name, source, width):
@@ -141,66 +143,72 @@ def tile_attend_gmf_sq_v_kb_kernel(tc, uT, vT, y, us, ts, kb, offs, uoffs, out):
             at = (b * PACK + j) * P
             gather(on_scalar, w_picked[:, at:at + P], v_win[j], slots(b * P, (b + 1) * P))
 
-        def pick_item_plane(j):
-            blocks = w_picked[:].rearrange("p (b j i) -> p j b i", b=NB, j=PACK)[:, j]
-            gather(False, blocks, v_win[j], items[:])
+        def pick_item_blocks(j, count):
+            blocks = w_picked[:].rearrange("p (b j i) -> p j b i", b=NB, j=PACK)[:, j, :count]
+            gather(False, blocks, v_win[j], slots(0, count * P))
 
         def weave_items(b, on_scalar):
             w_bf[b] = keep.tile([P, PASS], BF16, name=f"w_bf{b}", align_bytes=64)
-            weave(on_scalar, w_bf[b][:].rearrange("p (c i j) -> p c j i", i=RUN, j=PACK),
+            move(on_scalar, w_bf[b][:].rearrange("p (c i j) -> p c j i", i=RUN, j=PACK),
                   w_picked[:, b * PASS:(b + 1) * PASS].rearrange("p (j c i) -> p c j i", j=PACK, i=RUN))
 
-        def clear_window(j):
-            out_win.append(keep.tile([P, T], F32, name=f"out_win{j}", tag=f"u_win{j - 1}"))
-            nc.gpsimd.memset(out_win[j][:], 0.0)
+        tiles = [(2 * h + k, g) for h in range(2) for g in range(G) for k in range(2)]
+        count = len(tiles)
+        by_table = [n for n in range(count) if KINDS[n] == "t"]
 
         spread_us(0)
         spread_us(1)
         neg_ts = negated_column("ts", ts_win, True)
-        pick_users(0, False)
-        clear_window(1)
-        pick_users(1, False)
-        clear_window(2)
+        pick_users(0, 0, R, False)
+        pick_users(1, 0, R, False)
         neg_kb = negated_column("kb", kb_win, True)
         ts_sq = keep.tile([P, NB], F32, name="ts_sq")
         ts_kb = keep.tile([P, NB], F32, name="ts_kb")
         nc.gpsimd.tensor_tensor(ts_sq[:], neg_ts[:], neg_ts[:], ALU.mult)
         nc.gpsimd.tensor_tensor(ts_kb[:], neg_ts[:], neg_kb[:], ALU.mult)
-        pick_users(2, False)
-        clear_window(3)
-        turn_users(0)
-        turn_users(1)
-        pick_users(3, True)
-        pick_item_plane(0)
+        neg_c = {}
+        for n in by_table:
+            b, g = tiles[n]
+            neg_c[n] = keep.tile([P, PACK, P], F32, name=f"neg_c{n}")
+            nc.gpsimd.tensor_scalar(neg_c[n][:], us_rows[g][:], neg_ts[:, b:b + 1], 0.0, ALU.mult, ALU.add)
+        for j in range(2, PACK):
+            pick_users(j, 0, PASS, False)
+            pick_users(j, PASS, R, True)
+        xt_bf = keep.tile([P, G * D * PACK], BF16, name="xt_bf", tag=f"u_win{PACK - 1}", align_bytes=64)
         weave_users(0, False)
-        turn_users(2)
-        turn_users(3)
-        for b in range(NB):
-            pick_items(1, b, True)
-        x_codes[0], x_scales[0] = quantise("x0", x_bf[0][:], PASS)
+        for j in range(PACK):
+            turn_users(j)
+        pick_item_blocks(0, NB)
         weave_users(1, True)
+        x_codes[0], x_scales[0] = quantise("x0", x_bf[0][:], PASS)
+        pick_item_blocks(1, NB)
         xt_codes, xt_scales = quantise("xt", xt_bf[:], G * D)
-        pick_item_plane(2)
         x_codes[1], x_scales[1] = quantise("x1", x_bf[1][:], PASS)
-        pick_items(3, 0, False)
-        pick_items(3, 1, True)
-        weave_items(0, False)
-        weave_items(1, True)
+        pick_item_blocks(2, 2)
+        for b in range(2, NB):
+            pick_items(2, b, True)
+        for b in range(NB):
+            pick_items(3, b, b >= 2)
+        for b in range(NB):
+            weave_items(b, b >= 2)
         for b in range(2):
             w_codes[b], w_scales[b] = quantise(f"w{b}", w_bf[b][:], P)
 
         h_codes = [keep.tile([P, N], U32, name=f"h_codes{g}", align_bytes=64) for g in range(G)]
         h_scales = [keep.tile([P, N], U8, name=f"h_scales{g}", align_bytes=64) for g in range(G)]
-        tiles = [(2 * h + k, g) for h in range(2) for g in range(G) for k in range(2)]
-        targets, a_banks, scaled, z_banks, h_bf = {}, {}, {}, {}, {}
+        y_banks, targets, a_banks, scaled, z_banks, h_bf, pairs_of = {}, {}, {}, {}, {}, {}, {}
 
-        def target_term(n):
+        def turn_targets(n):
             b, g = tiles[n]
-            bank = psum.tile([P, PASS], F32, name="y_bank", tag="y_bank")
+            if n in by_table:
+                y_banks[n] = psum.tile([P, PASS], F32, name="y_bank", tag="y_bank")
+            else:
+                y_banks[n] = psum.tile([P, PASS], F32, name="y_brief", tag="d_bank", bufs=1)
             for t in range(PACK):
-                nc.tensor.transpose(bank[:, t * P:(t + 1) * P], y_sb[(b // 2, g)][:, t, (b % 2) * P:(b % 2 + 1) * P], ident[:])
-            targets[n] = work.tile([P, PASS], F32, name="target", bufs=4)
-            nc.scalar.activation(out=targets[n][:], in_=bank[:], func=IDENTITY, scale=neg_ts[:, b:b + 1], bias=ts_kb[:, b:b + 1])
+                nc.tensor.transpose(y_banks[n][:, t * P:(t + 1) * P], y_sb[(b // 2, g)][:, t, (b % 2) * P:(b % 2 + 1) * P], ident[:])
+            if n not in by_table:
+                targets[n] = work.tile([P, PASS], F32, name="target", bufs=4)
+                nc.scalar.activation(out=targets[n][:], in_=y_banks[n][:], func=IDENTITY, scale=neg_ts[:, b:b + 1], bias=ts_kb[:, b:b + 1])
 
         def scores(n):
             b, g = tiles[n]
@@ -210,12 +218,13 @@ def tile_attend_gmf_sq_v_kb_kernel(tc, uT, vT, y, us, ts, kb, offs, uoffs, out):
 
         def score_term(n):
             b, g = tiles[n]
-            scaled[n] = work.tile([P, PACK, P], F32, name="scaled", tag="scaled")
-            nc.vector.scalar_tensor_tensor(scaled[n][:], a_banks[n][:].rearrange("p (s t) -> p t s", t=PACK), ts_sq[:, b:b + 1],
+            factor = neg_ts if n in by_table else ts_sq
+            scaled[n] = work.tile([P, PACK, P], F32, name="scaled", bufs=4)
+            nc.vector.scalar_tensor_tensor(scaled[n][:], a_banks[n][:].rearrange("p (s t) -> p t s", t=PACK), factor[:, b:b + 1],
                                            us_rows[g][:], ALU.mult, ALU.mult)
 
         def add_terms(n):
-            z_banks[n] = psum.tile([P, PACK, P], F32, name="z_bank", tag="z_bank")
+            z_banks[n] = psum.tile([P, PACK, P], F32, name="z_bank", tag="z_bank" if n < count - 2 else "y_bank")
             for t in range(PACK):
                 nc.tensor.matmul(z_banks[n][:, t, :], targets[n][:, t * P:(t + 1) * P], ident[:], start=(t == 0), stop=False, is_transpose=True)
             for t in range(PACK):
@@ -223,15 +232,34 @@ def tile_attend_gmf_sq_v_kb_kernel(tc, uT, vT, y, us, ts, kb, offs, uoffs, out):
 
         def round_h(n):
             b, g = tiles[n]
-            h_bf[n] = work.tile([P, P, PACK], BF16, name="h_bf", align_bytes=64)
-            nc.vector.tensor_tensor(h_bf[n][:], z_banks[n][:].rearrange("s t i -> s i t"),
+            if n == count - 1:
+                h_bf[n] = keep.tile([P, P * PACK], BF16, name="h_last", tag="h_last", align_bytes=64)
+            else:
+                h_bf[n] = work.tile([P, P * PACK], BF16, name="h_bf", tag="h_bf", align_bytes=64, bufs=4)
+            nc.vector.tensor_tensor(h_bf[n][:].rearrange("s (i t) -> s i t", t=PACK), z_banks[n][:].rearrange("s t i -> s i t"),
                                     us_col[:, g:g + 1, :].to_broadcast([P, P, PACK]), ALU.mult)
+
+        def round_h_by_table(n):
+            b, g = tiles[n]
+            resid = work.tile([P, PASS], F32, name="resid")
+            nc.vector.scalar_tensor_tensor(resid[:], scaled[n][:].rearrange("p t s -> p (t s)"), neg_kb[:, b:b + 1], y_banks[n][:], ALU.add, ALU.add)
+            pairs = work.tile([P, 2, P, 2], BF16, name="pairs")
+            pairs_of[n] = pairs
+            nc.gpsimd.tensor_tensor(pairs[:], resid[:].rearrange("p (u e s) -> p u s e", u=2, e=2),
+                                    neg_c[n][:].rearrange("p (u e) s -> p u s e", e=2), ALU.mult)
+
+        def turn_h(n):
+            words = pairs_of[n][:].rearrange("p u s e -> p (u s e)").bitcast(F32)
+            bank = psum.tile([P, 2, P], F32, name="h_bank", bufs=1)
+            for u in range(2):
+                nc.tensor.transpose(bank[:, u, :], words[:, u * P:(u + 1) * P], ident[:])
+            h_bf[n] = work.tile([P, P * PACK], BF16, name="h_bf", tag="h_bf", align_bytes=64, bufs=4)
+            nc.scalar.copy(out=h_bf[n][:].bitcast(F32).rearrange("s (i u) -> s i u", u=2), in_=bank[:].rearrange("s u i -> s i u"))
 
         def quantise_h(n):
             b, g = tiles[n]
             cols = slice(b * P, (b + 1) * P)
-            nc.vector.quantize_mx(out=h_codes[g][:, cols].bitcast(E5M2), scales=h_scales[g][:, cols],
-                                  in_=h_bf[n][:].rearrange("s i t -> s (i t)"))
+            nc.vector.quantize_mx(out=h_codes[g][:, cols].bitcast(E5M2), scales=h_scales[g][:, cols], in_=h_bf[n][:])
 
         def gradient(j, lo, hi, bank):
             for g in range(G):
@@ -241,40 +269,47 @@ def tile_attend_gmf_sq_v_kb_kernel(tc, uT, vT, y, us, ts, kb, offs, uoffs, out):
                                     start=(g == 0), stop=(g == G - 1))
 
         out_planes = out.rearrange("(p j) c -> j p c", j=PACK)
-        count = len(tiles)
-        for n in range(2):
-            target_term(n)
+        for n in range(3):
+            if n < 2 or n not in by_table:
+                turn_targets(n)
         for n in range(2):
             scores(n)
-        for b in range(2, NB):
-            pick_items(3, b, True)
-            weave_items(b, True)
+        done = []
         for n in range(count + 3):
             if n < count:
                 score_term(n)
+            if n == 1:
+                for b in range(2, NB):
+                    w_codes[b], w_scales[b] = quantise(f"w{b}", w_bf[b][:], P)
             if n + 2 < count:
-                target_term(n + 2)
-                if n + 2 == count // 2:
-                    for b in range(2, NB):
-                        w_codes[b], w_scales[b] = quantise(f"w{b}", w_bf[b][:], P)
                 scores(n + 2)
-            if n < count:
+            if n < count and n not in by_table:
                 add_terms(n)
+            if n - 3 in by_table:
+                turn_h(n - 3)
             if 0 <= n - 2 < count:
-                round_h(n - 2)
-            if 0 <= n - 3 < count:
-                quantise_h(n - 3)
-            if n - 3 == count // 2 - 1:
-                early = psum.tile([P, 2, HALF], F32, name="early", tag="d_bank")
-                for j in range(2):
-                    gradient(j, 0, HALF, early[:, j, :])
-                early0 = keep.tile([P, HALF], F32, name="early0")
-                nc.scalar.copy(out=early0[:], in_=early[:, 0, :])
-                scatter(True, out_win[0], slots(0, HALF), early0[:])
-            if n == count - 1:
-                early1 = work.tile([P, HALF], F32, name="early1", tag="scaled")
-                nc.scalar.copy(out=early1[:], in_=early[:, 1, :])
+                if n - 2 in by_table:
+                    round_h_by_table(n - 2)
+                else:
+                    round_h(n - 2)
+            if n >= 2 and n in by_table:
+                turn_targets(n)
+            if n + 4 < count and n + 4 not in by_table:
+                turn_targets(n + 4)
+            for m in range(count):
+                if m not in done and n - 2 >= m + (2 if m in by_table else 1):
+                    quantise_h(m)
+                    done.append(m)
+                    if all(k in done for k in range(count // 2)) and m < count // 2:
+                        early = psum.tile([P, 2, HALF], F32, name="early", tag="d_bank", bufs=1)
+                        for j in range(2):
+                            gradient(j, 0, HALF, early[:, j, :])
+                        early0 = keep.tile([P, HALF], F32, name="early0")
+                        nc.scalar.copy(out=early0[:], in_=early[:, 0, :])
+                        scatter(True, out_win[0], slots(0, HALF), early0[:])
 
+        early1 = keep.tile([P, HALF], F32, name="early1", tag="h_last", align_bytes=64)
+        nc.vector.tensor_copy(early1[:], early[:, 1, :])
         scatter(False, out_win[1], slots(0, HALF), early1[:])
         for j in range(PACK):
             lo = HALF if j < 2 else 0
@@ -282,7 +317,7 @@ def tile_attend_gmf_sq_v_kb_kernel(tc, uT, vT, y, us, ts, kb, offs, uoffs, out):
             gradient(j, lo, N, bank[:])
             staged = keep.tile([P, N - lo], F32, name=f"staged{j}")
             on_scalar = j % 2 == 0
-            weave(on_scalar, staged[:], bank[:])
+            move(on_scalar, staged[:], bank[:])
             if j == 2:
                 for h in range(2):
                     scatter(True, out_win[j], slots(h * HALF, (h + 1) * HALF), staged[:, h * HALF:(h + 1) * HALF])

@@ -39,14 +39,11 @@ def tile_attend_gmf_sq_v_kb_kernel(tc, uT, vT, y, us, ts, kb, offs, uoffs, out):
 
         ident = keep.tile([P, P], F32, name="ident")
         make_identity(nc, ident[:])
-        ts_win = keep.tile([P, T], F32, name="ts_win")
+        ts_win = keep.tile([P, T], F32, name="ts_win", tag="ts_win", align_bytes=64)
         kb_win = keep.tile([P, T], F32, name="kb_win")
-        out_win = []
+        out_win = {}
         for win in (ts_win, kb_win):
             nc.vector.memset(win[:LIVE, :], 0.0)
-        for j in range(PACK):
-            out_win.append(keep.tile([P, T], F32, name=f"out_win{j}"))
-            nc.gpsimd.memset(out_win[j][:], 0.0)
 
         items = keep.tile([P, N // PER_COLUMN], U16, name="items")
         users = keep.tile([P, R // PER_COLUMN], U16, name="users")
@@ -98,8 +95,8 @@ def tile_attend_gmf_sq_v_kb_kernel(tc, uT, vT, y, us, ts, kb, offs, uoffs, out):
             nc.scalar.activation(out=col[:], in_=turned[:, :, LIVE], func=COPY, scale=-1.0)
             return col
 
-        x_picked = keep.tile([P, PACK * R], BF16, name="x_picked")
-        w_picked = keep.tile([P, PACK * N], BF16, name="w_picked")
+        x_picked = keep.tile([P, PACK * R], BF16, name="x_picked", tag="x_picked")
+        w_picked = keep.tile([P, PACK * N], BF16, name="w_picked", tag="w_picked")
         us_rows, x_bf, w_bf = {}, {}, {}
         x_codes, x_scales, w_codes, w_scales = {}, {}, {}, {}
 
@@ -152,6 +149,18 @@ def tile_attend_gmf_sq_v_kb_kernel(tc, uT, vT, y, us, ts, kb, offs, uoffs, out):
             move(on_scalar, w_bf[b][:].rearrange("p (c i j) -> p c j i", i=RUN, j=PACK),
                   w_picked[:, b * PASS:(b + 1) * PASS].rearrange("p (j c i) -> p c j i", j=PACK, i=RUN))
 
+        neg_c = {}
+
+        def scale_tables(g, tag):
+            pair = keep.tile([P, 2 * PASS], F32, name=f"neg_c{g}", tag=tag)
+            for b in range(2):
+                neg_c[2 * g + b] = pair[:, b * PASS:(b + 1) * PASS]
+                nc.scalar.activation(out=neg_c[2 * g + b], in_=us_rows[g][:].rearrange("p t s -> p (t s)"), func=COPY, scale=neg_ts[:, b:b + 1])
+
+        def clear_window(j, tag):
+            out_win[j] = keep.tile([P, T], F32, name=f"out_win{j}", tag=tag, align_bytes=64)
+            nc.gpsimd.memset(out_win[j][:], 0.0)
+
         tiles = [(2 * h + k, g) for h in range(2) for g in range(G) for k in range(2)]
         count = len(tiles)
         by_table = [n for n in range(count) if KINDS[n] == "t"]
@@ -159,18 +168,15 @@ def tile_attend_gmf_sq_v_kb_kernel(tc, uT, vT, y, us, ts, kb, offs, uoffs, out):
         spread_us(0)
         spread_us(1)
         neg_ts = negated_column("ts", ts_win, True)
+        clear_window(0, "ts_win")
         pick_users(0, 0, R, False)
+        clear_window(1, "u_win0")
         pick_users(1, 0, R, False)
         neg_kb = negated_column("kb", kb_win, True)
         ts_sq = keep.tile([P, NB], F32, name="ts_sq")
         ts_kb = keep.tile([P, NB], F32, name="ts_kb")
         nc.gpsimd.tensor_tensor(ts_sq[:], neg_ts[:], neg_ts[:], ALU.mult)
         nc.gpsimd.tensor_tensor(ts_kb[:], neg_ts[:], neg_kb[:], ALU.mult)
-        neg_c = {}
-        for n in by_table:
-            b, g = tiles[n]
-            neg_c[n] = keep.tile([P, PACK, P], F32, name=f"neg_c{n}")
-            nc.gpsimd.tensor_scalar(neg_c[n][:], us_rows[g][:], neg_ts[:, b:b + 1], 0.0, ALU.mult, ALU.add)
         for j in range(2, PACK):
             pick_users(j, 0, PASS, False)
             pick_users(j, PASS, R, True)
@@ -187,12 +193,16 @@ def tile_attend_gmf_sq_v_kb_kernel(tc, uT, vT, y, us, ts, kb, offs, uoffs, out):
         pick_item_blocks(2, 2)
         for b in range(2, NB):
             pick_items(2, b, True)
-        for b in range(NB):
-            pick_items(3, b, b >= 2)
-        for b in range(NB):
-            weave_items(b, b >= 2)
+        scale_tables(0, "x_picked")
+        for b in range(2):
+            pick_items(3, b, b > 0)
+            weave_items(b, b > 0)
         for b in range(2):
             w_codes[b], w_scales[b] = quantise(f"w{b}", w_bf[b][:], P)
+        for b in range(2, NB):
+            pick_items(3, b, True)
+            weave_items(b, True)
+        scale_tables(1, "w_picked")
 
         h_codes = [keep.tile([P, N], U32, name=f"h_codes{g}", align_bytes=64) for g in range(G)]
         h_scales = [keep.tile([P, N], U8, name=f"h_scales{g}", align_bytes=64) for g in range(G)]
@@ -200,10 +210,12 @@ def tile_attend_gmf_sq_v_kb_kernel(tc, uT, vT, y, us, ts, kb, offs, uoffs, out):
 
         def turn_targets(n):
             b, g = tiles[n]
-            if n in by_table:
+            if n <= count // 2:
                 y_banks[n] = psum.tile([P, PASS], F32, name="y_bank", tag="y_bank")
+            elif n < count - 1:
+                y_banks[n] = psum.tile([P, PASS], F32, name="y_brief", tag="z_bank")
             else:
-                y_banks[n] = psum.tile([P, PASS], F32, name="y_brief", tag="d_bank", bufs=1)
+                y_banks[n] = psum.tile([P, PASS], F32, name="y_last", tag="d_bank", bufs=1)
             for t in range(PACK):
                 nc.tensor.transpose(y_banks[n][:, t * P:(t + 1) * P], y_sb[(b // 2, g)][:, t, (b % 2) * P:(b % 2 + 1) * P], ident[:])
             if n not in by_table:
@@ -232,8 +244,8 @@ def tile_attend_gmf_sq_v_kb_kernel(tc, uT, vT, y, us, ts, kb, offs, uoffs, out):
 
         def round_h(n):
             b, g = tiles[n]
-            if n == count - 1:
-                h_bf[n] = keep.tile([P, P * PACK], BF16, name="h_last", tag="h_last", align_bytes=64)
+            if n >= count - 2:
+                h_bf[n] = keep.tile([P, P * PACK], BF16, name=f"h_late{n}", tag=f"h_late{n}", align_bytes=64)
             else:
                 h_bf[n] = work.tile([P, P * PACK], BF16, name="h_bf", tag="h_bf", align_bytes=64, bufs=4)
             nc.vector.tensor_tensor(h_bf[n][:].rearrange("s (i t) -> s i t", t=PACK), z_banks[n][:].rearrange("s t i -> s i t"),
@@ -246,7 +258,7 @@ def tile_attend_gmf_sq_v_kb_kernel(tc, uT, vT, y, us, ts, kb, offs, uoffs, out):
             pairs = work.tile([P, 2, P, 2], BF16, name="pairs")
             pairs_of[n] = pairs
             nc.gpsimd.tensor_tensor(pairs[:], resid[:].rearrange("p (u e s) -> p u s e", u=2, e=2),
-                                    neg_c[n][:].rearrange("p (u e) s -> p u s e", e=2), ALU.mult)
+                                    neg_c[n].rearrange("p (u e s) -> p u s e", u=2, e=2), ALU.mult)
 
         def turn_h(n):
             words = pairs_of[n][:].rearrange("p u s e -> p (u s e)").bitcast(F32)
@@ -269,48 +281,50 @@ def tile_attend_gmf_sq_v_kb_kernel(tc, uT, vT, y, us, ts, kb, offs, uoffs, out):
                                     start=(g == 0), stop=(g == G - 1))
 
         out_planes = out.rearrange("(p j) c -> j p c", j=PACK)
-        for n in range(3):
-            if n < 2 or n not in by_table:
-                turn_targets(n)
+        for n in range(2):
+            turn_targets(n)
         for n in range(2):
             scores(n)
-        done = []
+        half = count // 2
         for n in range(count + 3):
             if n < count:
                 score_term(n)
-            if n == 1:
+            if n == 2:
                 for b in range(2, NB):
                     w_codes[b], w_scales[b] = quantise(f"w{b}", w_bf[b][:], P)
             if n + 2 < count:
                 scores(n + 2)
-            if n < count and n not in by_table:
+            if half <= n - 1 < count - 1:
+                add_terms(n - 1)
+            if n == count - 1:
                 add_terms(n)
-            if n - 3 in by_table:
+                quantise_h(half - 1)
+                early = psum.tile([P, 2, HALF], F32, name="early", tag="d_bank", bufs=1)
+                for j in range(2):
+                    gradient(j, 0, HALF, early[:, j, :])
+                early0 = keep.tile([P, HALF], F32, name="early0")
+                nc.scalar.copy(out=early0[:], in_=early[:, 0, :])
+                scatter(True, out_win[0], slots(0, HALF), early0[:])
+            if 0 <= n - 3 < half:
                 turn_h(n - 3)
-            if 0 <= n - 2 < count:
-                if n - 2 in by_table:
-                    round_h_by_table(n - 2)
-                else:
-                    round_h(n - 2)
-            if n >= 2 and n in by_table:
+            if 0 <= n - 2 < half:
+                round_h_by_table(n - 2)
+            if half <= n - 2 < count:
+                round_h(n - 2)
+            if 2 <= n <= half:
                 turn_targets(n)
-            if n + 4 < count and n + 4 not in by_table:
+            if half < n + 4 < count:
                 turn_targets(n + 4)
-            for m in range(count):
-                if m not in done and n - 2 >= m + (2 if m in by_table else 1):
-                    quantise_h(m)
-                    done.append(m)
-                    if all(k in done for k in range(count // 2)) and m < count // 2:
-                        early = psum.tile([P, 2, HALF], F32, name="early", tag="d_bank", bufs=1)
-                        for j in range(2):
-                            gradient(j, 0, HALF, early[:, j, :])
-                        early0 = keep.tile([P, HALF], F32, name="early0")
-                        nc.scalar.copy(out=early0[:], in_=early[:, 0, :])
-                        scatter(True, out_win[0], slots(0, HALF), early0[:])
+            if 0 <= n - 4 < half - 1:
+                quantise_h(n - 4)
+            if half <= n - 3 < count:
+                quantise_h(n - 3)
 
-        early1 = keep.tile([P, HALF], F32, name="early1", tag="h_last", align_bytes=64)
+        clear_window(2, f"h_late{count - 1}")
+        early1 = keep.tile([P, HALF], F32, name="early1", tag=f"h_late{count - 2}", align_bytes=64)
         nc.vector.tensor_copy(early1[:], early[:, 1, :])
         scatter(False, out_win[1], slots(0, HALF), early1[:])
+        clear_window(3, f"h_late{count - 2}")
         for j in range(PACK):
             lo = HALF if j < 2 else 0
             bank = psum.tile([P, N - lo], F32, name="dv_bank", tag="y_bank" if j < 2 else "a_bank")

@@ -157,20 +157,22 @@ def tile_attend_gmf_sq_v_kb_kernel(tc, uT, vT, y, us, ts, kb, offs, uoffs, out):
                 neg_c[2 * g + b] = pair[:, b * PASS:(b + 1) * PASS]
                 nc.scalar.activation(out=neg_c[2 * g + b], in_=us_rows[g][:].rearrange("p t s -> p (t s)"), func=COPY, scale=neg_ts[:, b:b + 1])
 
-        def clear_window(j, tag):
+        def clear_window(j, tag, engine):
             out_win[j] = keep.tile([P, T], F32, name=f"out_win{j}", tag=tag, align_bytes=64)
-            nc.gpsimd.memset(out_win[j][:], 0.0)
+            engine.memset(out_win[j][:], 0.0)
 
         tiles = [(2 * h + k, g) for h in range(2) for g in range(G) for k in range(2)]
         count = len(tiles)
         by_table = [n for n in range(count) if KINDS[n] == "t"]
 
+        for j in range(2, PACK):
+            clear_window(j, f"out_win{j}", nc.vector)
         spread_us(0)
         spread_us(1)
         neg_ts = negated_column("ts", ts_win, True)
-        clear_window(0, "ts_win")
+        clear_window(0, "ts_win", nc.gpsimd)
         pick_users(0, 0, R, False)
-        clear_window(1, "u_win0")
+        clear_window(1, "u_win0", nc.gpsimd)
         pick_users(1, 0, R, False)
         neg_kb = negated_column("kb", kb_win, True)
         ts_sq = keep.tile([P, NB], F32, name="ts_sq")
@@ -320,11 +322,9 @@ def tile_attend_gmf_sq_v_kb_kernel(tc, uT, vT, y, us, ts, kb, offs, uoffs, out):
             if half <= n - 3 < count:
                 quantise_h(n - 3)
 
-        clear_window(2, f"h_late{count - 1}")
         early1 = keep.tile([P, HALF], F32, name="early1", tag=f"h_late{count - 2}", align_bytes=64)
         nc.vector.tensor_copy(early1[:], early[:, 1, :])
         scatter(False, out_win[1], slots(0, HALF), early1[:])
-        clear_window(3, f"h_late{count - 2}")
         for j in range(PACK):
             lo = HALF if j < 2 else 0
             bank = psum.tile([P, N - lo], F32, name="dv_bank", tag="y_bank" if j < 2 else "a_bank")

from contextlib import ExitStack

import concourse.mybir as mybir
from concourse.masks import make_identity

D, T, TU, N, R = 512, 2048, 2048, 512, 1024
P = 128
PACK = 4
PASS = P * PACK
G = R // PASS
NB = N // P
HALF = N // 2
RUN = 4
PER_COLUMN = 16
LIVE = P - 1
KINDS = "ttttssss"

FLOPS = 2 * 2 * R * N * D
BYTES = 4 * (D * TU + D * T + R * N + R + 2 * T + D * T) + 2 * P * (N + R) // 16

F32 = mybir.dt.float32
BF16 = mybir.dt.bfloat16
U32 = mybir.dt.uint32
U16 = mybir.dt.uint16
U8 = mybir.dt.uint8
E4M3 = mybir.dt.float8_e4m3fn_x4
E5M2 = mybir.dt.float8_e5m2_x4
ALU = mybir.AluOpType
COPY = mybir.ActivationFunctionType.Copy
IDENTITY = mybir.ActivationFunctionType.Identity


def tile_attend_gmf_sq_v_kb_kernel(tc, uT, vT, y, us, ts, kb, offs, uoffs, out):
    nc = tc.nc
    with ExitStack() as ctx:
        keep = ctx.enter_context(tc.tile_pool(name="keep", bufs=1))
        work = ctx.enter_context(tc.tile_pool(name="work", bufs=3))
        psum = ctx.enter_context(tc.psum_pool(name="psum", bufs=2))

        ident = keep.tile([P, P], F32, name="ident")
        make_identity(nc, ident[:])
        ts_win = keep.tile([P, T], F32, name="ts_win", tag="ts_win", align_bytes=64)
        kb_win = keep.tile([P, T], F32, name="kb_win")
        out_win = {}
        for win in (ts_win, kb_win):
            nc.vector.memset(win[:LIVE, :], 0.0)

        items = keep.tile([P, N // PER_COLUMN], U16, name="items")
        users = keep.tile([P, R // PER_COLUMN], U16, name="users")
        us_col = keep.tile([P, G, PACK], F32, name="us_col")
        u_planes = uT.rearrange("(p j) c -> j p c", j=PACK)
        v_planes = vT.rearrange("(p j) c -> j p c", j=PACK)
        u_win = [keep.tile([P, TU], F32, name=f"u_win{j}", tag=f"u_win{j}", align_bytes=64) for j in range(PACK)]
        v_win = [keep.tile([P, T], F32, name=f"v_win{j}") for j in range(PACK)]
        nc.scalar.dma_start(out=us_col[:], in_=us[0].rearrange("(g s t) o -> s g (t o)", g=G, t=PACK))
        nc.scalar.dma_start(out=ts_win[LIVE:, :], in_=ts[0:1, :])
        nc.scalar.dma_start(out=kb_win[LIVE:, :], in_=kb[0:1, :])
        nc.sync.dma_start(out=u_win[0][:], in_=u_planes[0])
        nc.sync.dma_start(users[:], uoffs)
        nc.sync.dma_start(items[:], offs)
        nc.sync.dma_start(out=u_win[1][:], in_=u_planes[1])
        for j in range(2, PACK):
            nc.sync.dma_start(out=u_win[j][:], in_=u_planes[j])
        for j in range(PACK):
            nc.sync.dma_start(out=v_win[j][:], in_=v_planes[j])
        y_sb = {}
        for h in range(2):
            for g in range(G):
                y_sb[(h, g)] = keep.tile([P, PACK, HALF], F32, name=f"y_sb{h}_{g}")
                nc.sync.dma_start(out=y_sb[(h, g)][:],
                                  in_=y[0, g * PASS:(g + 1) * PASS, h * HALF:(h + 1) * HALF].rearrange("(s t) i -> s t i", t=PACK))

        def gather(on_scalar, dst, win, offsets):
            if on_scalar:
                nc.scalar.activation(out=dst, in_=win[:].indirect(offsets), func=COPY)
            else:
                nc.vector.tensor_copy(dst, win[:].indirect(offsets))

        def scatter(on_scalar, win, offsets, src):
            if on_scalar:
                nc.scalar.activation(out=win[:].indirect(offsets), in_=src, func=COPY)
            else:
                nc.vector.tensor_copy(win[:].indirect(offsets), src)

        def slots(lo, hi):
            return items[:, lo // PER_COLUMN:hi // PER_COLUMN]

        def negated_column(name, win, on_scalar):
            picked = keep.tile([P, N], F32, name=f"{name}_picked")
            gather(on_scalar, picked[:], win, items[:])
            turned = psum.tile([P, NB, P], F32, name="turned", tag="y_bank")
            for b in range(NB):
                nc.tensor.transpose(turned[:, b, :], picked[:, b * P:(b + 1) * P], ident[:])
            col = keep.tile([P, NB], F32, name=f"neg_{name}")
            nc.scalar.activation(out=col[:], in_=turned[:, :, LIVE], func=COPY, scale=-1.0)
            return col

        x_picked = keep.tile([P, PACK * R], BF16, name="x_picked", tag="x_picked")
        w_picked = keep.tile([P, PACK * N], BF16, name="w_picked", tag="w_picked")
        us_rows, x_bf, w_bf = {}, {}, {}
        x_codes, x_scales, w_codes, w_scales = {}, {}, {}, {}

        def spread_us(g):
            bank = psum.tile([P, PACK, P], F32, name="us_bank", tag="z_bank")
            for t in range(PACK):
                nc.tensor.transpose(bank[:, t, :], us_col[:, g, t:t + 1].to_broadcast([P, P]), ident[:])
            us_rows[g] = keep.tile([P, PACK, P], F32, name=f"us_rows{g}")
            nc.scalar.activation(out=us_rows[g][:], in_=bank[:], func=COPY)

        def pick_users(j, lo, hi, on_scalar):
            gather(on_scalar, x_picked[:, j * R + lo:j * R + hi], u_win[j], users[:, lo // PER_COLUMN:hi // PER_COLUMN])

        def move(on_scalar, dst, src):
            if on_scalar:
                nc.scalar.copy(out=dst, in_=src)
            else:
                nc.vector.tensor_copy(dst, src)

        def turn_users(j):
            words = x_picked[:].bitcast(F32)[:, j * R // 2:(j + 1) * R // 2].rearrange("p (g s u) -> p g s u", g=G, u=2)
            bank = psum.tile([P, G, 2, P], F32, name="xt_bank", tag="a_bank" if j < 2 else "y_bank")
            for g in range(G):
                for u in range(2):
                    nc.tensor.transpose(bank[:, g, u, :], words[:, g, :, u], ident[:])
            nc.scalar.copy(out=xt_bf[:].bitcast(F32).rearrange("s (g j p u) -> s g j p u", g=G, j=PACK, u=2)[:, :, j],
                           in_=bank[:].rearrange("s g u p -> s g p u"))

        def weave_users(g, on_scalar):
            x_bf[g] = keep.tile([P, PASS * PACK], BF16, name=f"x_bf{g}", align_bytes=64)
            move(on_scalar, x_bf[g][:].rearrange("p (c i j) -> p c j i", i=RUN, j=PACK),
                  x_picked[:].rearrange("p (j g c i) -> p g c j i", j=PACK, g=G, i=RUN)[:, g])

        def quantise(name, source, width):
            codes = keep.tile([P, width], U32, name=f"{name}_codes", align_bytes=64)
            scales = keep.tile([P, width], U8, name=f"{name}_scales", align_bytes=64)
            nc.vector.quantize_mx(out=codes[:].bitcast(E4M3), scales=scales[:], in_=source)
            return codes, scales

        def pick_items(j, b, on_scalar):
            at = (b * PACK + j) * P
            gather(on_scalar, w_picked[:, at:at + P], v_win[j], slots(b * P, (b + 1) * P))

        def pick_item_blocks(j, count):
            blocks = w_picked[:].rearrange("p (b j i) -> p j b i", b=NB, j=PACK)[:, j, :count]
            gather(False, blocks, v_win[j], slots(0, count * P))

        def weave_items(b, on_scalar):
            w_bf[b] = keep.tile([P, PASS], BF16, name=f"w_bf{b}", align_bytes=64)
            move(on_scalar, w_bf[b][:].rearrange("p (c i j) -> p c j i", i=RUN, j=PACK),
                  w_picked[:, b * PASS:(b + 1) * PASS].rearrange("p (j c i) -> p c j i", j=PACK, i=RUN))

        neg_c = {}

        def scale_tables(g, tag):
            pair = keep.tile([P, 2 * PASS], F32, name=f"neg_c{g}", tag=tag)
            for b in range(2):
                neg_c[2 * g + b] = pair[:, b * PASS:(b + 1) * PASS]
                nc.scalar.activation(out=neg_c[2 * g + b], in_=us_rows[g][:].rearrange("p t s -> p (t s)"), func=COPY, scale=neg_ts[:, b:b + 1])

        def clear_window(j, tag, engine):
            out_win[j] = keep.tile([P, T], F32, name=f"out_win{j}", tag=tag, align_bytes=64)
            engine.memset(out_win[j][:], 0.0)

        tiles = [(2 * h + k, g) for h in range(2) for g in range(G) for k in range(2)]
        count = len(tiles)
        by_table = [n for n in range(count) if KINDS[n] == "t"]

        for j in range(2, PACK):
            clear_window(j, f"out_win{j}", nc.vector)
        spread_us(0)
        spread_us(1)
        neg_ts = negated_column("ts", ts_win, True)
        clear_window(0, "ts_win", nc.gpsimd)
        pick_users(0, 0, R, False)
        clear_window(1, "u_win0", nc.gpsimd)
        pick_users(1, 0, R, False)
        neg_kb = negated_column("kb", kb_win, True)
        ts_sq = keep.tile([P, NB], F32, name="ts_sq")
        ts_kb = keep.tile([P, NB], F32, name="ts_kb")
        nc.gpsimd.tensor_tensor(ts_sq[:], neg_ts[:], neg_ts[:], ALU.mult)
        nc.gpsimd.tensor_tensor(ts_kb[:], neg_ts[:], neg_kb[:], ALU.mult)
        for j in range(2, PACK):
            pick_users(j, 0, PASS, False)
            pick_users(j, PASS, R, True)
        xt_bf = keep.tile([P, G * D * PACK], BF16, name="xt_bf", tag=f"u_win{PACK - 1}", align_bytes=64)
        weave_users(0, False)
        for j in range(PACK):
            turn_users(j)
        pick_item_blocks(0, NB)
        weave_users(1, True)
        x_codes[0], x_scales[0] = quantise("x0", x_bf[0][:], PASS)
        pick_item_blocks(1, NB)
        xt_codes, xt_scales = quantise("xt", xt_bf[:], G * D)
        x_codes[1], x_scales[1] = quantise("x1", x_bf[1][:], PASS)
        pick_item_blocks(2, 2)
        for b in range(2, NB):
            pick_items(2, b, True)
        scale_tables(0, "x_picked")
        for b in range(2):
            pick_items(3, b, b > 0)
            weave_items(b, b > 0)
        for b in range(2):
            w_codes[b], w_scales[b] = quantise(f"w{b}", w_bf[b][:], P)
        for b in range(2, NB):
            pick_items(3, b, True)
            weave_items(b, True)
        scale_tables(1, "w_picked")

        h_codes = [keep.tile([P, N], U32, name=f"h_codes{g}", align_bytes=64) for g in range(G)]
        h_scales = [keep.tile([P, N], U8, name=f"h_scales{g}", align_bytes=64) for g in range(G)]
        y_banks, targets, a_banks, scaled, z_banks, h_bf, pairs_of = {}, {}, {}, {}, {}, {}, {}

        def turn_targets(n):
            b, g = tiles[n]
            if n <= count // 2:
                y_banks[n] = psum.tile([P, PASS], F32, name="y_bank", tag="y_bank")
            elif n < count - 1:
                y_banks[n] = psum.tile([P, PASS], F32, name="y_brief", tag="z_bank")
            else:
                y_banks[n] = psum.tile([P, PASS], F32, name="y_last", tag="d_bank", bufs=1)
            for t in range(PACK):
                nc.tensor.transpose(y_banks[n][:, t * P:(t + 1) * P], y_sb[(b // 2, g)][:, t, (b % 2) * P:(b % 2 + 1) * P], ident[:])
            if n not in by_table:
                targets[n] = work.tile([P, PASS], F32, name="target", bufs=4)
                nc.scalar.activation(out=targets[n][:], in_=y_banks[n][:], func=IDENTITY, scale=neg_ts[:, b:b + 1], bias=ts_kb[:, b:b + 1])

        def scores(n):
            b, g = tiles[n]
            a_banks[n] = psum.tile([P, PASS], F32, name="a_bank", tag="a_bank")
            nc.tensor.matmul_mx(out=a_banks[n][:], lhsT=w_codes[b][:].bitcast(E4M3), lhsT_scale=w_scales[b][:],
                                rhs=x_codes[g][:].bitcast(E4M3), rhs_scale=x_scales[g][:], start=True, stop=True)

        def score_term(n):
            b, g = tiles[n]
            factor = neg_ts if n in by_table else ts_sq
            scaled[n] = work.tile([P, PACK, P], F32, name="scaled", bufs=4)
            nc.vector.scalar_tensor_tensor(scaled[n][:], a_banks[n][:].rearrange("p (s t) -> p t s", t=PACK), factor[:, b:b + 1],
                                           us_rows[g][:], ALU.mult, ALU.mult)

        def add_terms(n):
            z_banks[n] = psum.tile([P, PACK, P], F32, name="z_bank", tag="z_bank" if n < count - 2 else "y_bank")
            for t in range(PACK):
                nc.tensor.matmul(z_banks[n][:, t, :], targets[n][:, t * P:(t + 1) * P], ident[:], start=(t == 0), stop=False, is_transpose=True)
            for t in range(PACK):
                nc.tensor.matmul(z_banks[n][:, t, :], scaled[n][:, t, :], ident[:], start=False, stop=(t == PACK - 1), is_transpose=True)

        def round_h(n):
            b, g = tiles[n]
            if n >= count - 2:
                h_bf[n] = keep.tile([P, P * PACK], BF16, name=f"h_late{n}", tag=f"h_late{n}", align_bytes=64)
            else:
                h_bf[n] = work.tile([P, P * PACK], BF16, name="h_bf", tag="h_bf", align_bytes=64, bufs=4)
            nc.vector.tensor_tensor(h_bf[n][:].rearrange("s (i t) -> s i t", t=PACK), z_banks[n][:].rearrange("s t i -> s i t"),
                                    us_col[:, g:g + 1, :].to_broadcast([P, P, PACK]), ALU.mult)

        def round_h_by_table(n):
            b, g = tiles[n]
            resid = work.tile([P, PASS], F32, name="resid")
            nc.vector.scalar_tensor_tensor(resid[:], scaled[n][:].rearrange("p t s -> p (t s)"), neg_kb[:, b:b + 1], y_banks[n][:], ALU.add, ALU.add)
            pairs = work.tile([P, 2, P, 2], BF16, name="pairs")
            pairs_of[n] = pairs
            nc.gpsimd.tensor_tensor(pairs[:], resid[:].rearrange("p (u e s) -> p u s e", u=2, e=2),
                                    neg_c[n].rearrange("p (u e s) -> p u s e", u=2, e=2), ALU.mult)

        def turn_h(n):
            words = pairs_of[n][:].rearrange("p u s e -> p (u s e)").bitcast(F32)
            bank = psum.tile([P, 2, P], F32, name="h_bank", bufs=1)
            for u in range(2):
                nc.tensor.transpose(bank[:, u, :], words[:, u * P:(u + 1) * P], ident[:])
            h_bf[n] = work.tile([P, P * PACK], BF16, name="h_bf", tag="h_bf", align_bytes=64, bufs=4)
            nc.scalar.copy(out=h_bf[n][:].bitcast(F32).rearrange("s (i u) -> s i u", u=2), in_=bank[:].rearrange("s u i -> s i u"))

        def quantise_h(n):
            b, g = tiles[n]
            cols = slice(b * P, (b + 1) * P)
            nc.vector.quantize_mx(out=h_codes[g][:, cols].bitcast(E5M2), scales=h_scales[g][:, cols], in_=h_bf[n][:])

        def gradient(j, lo, hi, bank):
            for g in range(G):
                at = g * D + j * P
                nc.tensor.matmul_mx(out=bank, lhsT=xt_codes[:, at:at + P].bitcast(E4M3), lhsT_scale=xt_scales[:, at:at + P],
                                    rhs=h_codes[g][:, lo:hi].bitcast(E5M2), rhs_scale=h_scales[g][:, lo:hi],
                                    start=(g == 0), stop=(g == G - 1))

        out_planes = out.rearrange("(p j) c -> j p c", j=PACK)
        for n in range(2):
            turn_targets(n)
        for n in range(2):
            scores(n)
        half = count // 2
        for n in range(count + 3):
            if n < count:
                score_term(n)
            if n == 2:
                for b in range(2, NB):
                    w_codes[b], w_scales[b] = quantise(f"w{b}", w_bf[b][:], P)
            if n + 2 < count:
                scores(n + 2)
            if half <= n - 1 < count - 1:
                add_terms(n - 1)
            if n == count - 1:
                add_terms(n)
                quantise_h(half - 1)
                early = psum.tile([P, 2, HALF], F32, name="early", tag="d_bank", bufs=1)
                for j in range(2):
                    gradient(j, 0, HALF, early[:, j, :])
                early0 = keep.tile([P, HALF], F32, name="early0")
                nc.scalar.copy(out=early0[:], in_=early[:, 0, :])
                scatter(True, out_win[0], slots(0, HALF), early0[:])
            if 0 <= n - 3 < half:
                turn_h(n - 3)
            if 0 <= n - 2 < half:
                round_h_by_table(n - 2)
            if half <= n - 2 < count:
                round_h(n - 2)
            if 2 <= n <= half:
                turn_targets(n)
            if half < n + 4 < count:
                turn_targets(n + 4)
            if 0 <= n - 4 < half - 1:
                quantise_h(n - 4)
            if half <= n - 3 < count:
                quantise_h(n - 3)

        early1 = keep.tile([P, HALF], F32, name="early1", tag=f"h_late{count - 2}", align_bytes=64)
        nc.vector.tensor_copy(early1[:], early[:, 1, :])
        scatter(False, out_win[1], slots(0, HALF), early1[:])
        for j in range(PACK):
            lo = HALF if j < 2 else 0
            bank = psum.tile([P, N - lo], F32, name="dv_bank", tag="y_bank" if j < 2 else "a_bank")
            gradient(j, lo, N, bank[:])
            staged = keep.tile([P, N - lo], F32, name=f"staged{j}")
            on_scalar = j % 2 == 0
            move(on_scalar, staged[:], bank[:])
            if j == 2:
                for h in range(2):
                    scatter(True, out_win[j], slots(h * HALF, (h + 1) * HALF), staged[:, h * HALF:(h + 1) * HALF])
            else:
                scatter(on_scalar, out_win[j], slots(lo, N), staged[:])
            nc.sync.dma_start(out=out_planes[j], in_=out_win[j][:])
